import numpy as np, ml_dtypes
CORES = [23,119,17,113]
N = 4
import mx_ref
BF = ml_dtypes.bfloat16
def tile(rs):
    return np.stack(rs, axis=2).reshape(128, -1).astype(BF)
def cut(t, i, w=512):
    return t[:, w * i:w * i + w]
def pick(q, e):
    c = np.concatenate([q[0].reshape(128, -1, 4), np.zeros((128, 1, 4), np.uint8)], axis=1); s = np.concatenate([q[1], np.ones((16, 1), np.uint8)], axis=1)
    return (np.ascontiguousarray(c[:, e].reshape(128, -1)), np.ascontiguousarray(s[:, e]))
def join(*qs):
    return (np.concatenate([q[0] for q in qs], axis=1), np.concatenate([q[1] for q in qs], axis=1))
def put(q, e, v):
    c, s = q[0].reshape(128, -1, 4).copy(), q[1].copy(); c[:, e] = v[0].reshape(128, -1, 4); s[:, e] = v[1]
    return (c.reshape(128, -1), s)
def pk(c, s):
    return (np.ascontiguousarray(c), mx_ref.live(s))
def emit(q):
    return q[0], q[1]
def packed(v, rng):
    q = [mx_ref.quantize(np.ascontiguousarray(v[r])) for r in range(N)]
    return np.stack([a for a, b in q]), np.stack([mx_ref.plane(b, rng) for a, b in q])
def values_of_codes():
    e, c = np.zeros((128, 128, 4), np.float32), np.zeros((128, 2, 4), np.uint8)
    e[np.arange(128), np.arange(128), 0] = 1
    c[:127, :, 0] = np.arange(256).reshape(2, 128).T[:127]
    return mx_ref.matmul(mx_ref.quantize(e.reshape(128, 512).astype(BF)), (c.reshape(128, 8), np.full((16, 2), 127, np.uint8))).T.reshape(-1).astype(np.float64)
CODE_VALUE, SCALE_VALUE = values_of_codes(), 2.0 ** (np.arange(256) - 127.0)
def decode(q):
    return (CODE_VALUE[q[0]].reshape(16, 8, -1, 4) * SCALE_VALUE[q[1]][:, None, :, None] + 0.0).reshape(128, -1).astype(np.float32)
def f(rng, *shape):
    return mx_ref.flush((rng.standard_normal(shape, dtype=np.float32) * np.exp2(rng.integers(-2, 3, shape[:-1] + (1,)))).astype(BF))
def wide(rng, *shape, cols=0):
    v = rng.standard_normal(shape, dtype=np.float32) * np.exp2(rng.integers(-12, 13, shape)).astype(np.float32)
    if cols: v *= np.repeat(np.exp2(rng.integers(-cols, cols + 1, shape[:-2] + (1, shape[-1] // 4))) * (rng.random(shape[:-2] + (1, shape[-1] // 4)) > 0.0625), 4, axis=-1).astype(np.float32)
    return mx_ref.flush(v.astype(BF))
C, B, K, R = 384, 5, 32, 2
def key_of(s):
    b = (s.reshape(8, 16, C)[:, :B] < 0).astype(np.int64)
    return np.sum(b << np.arange(B)[:, None], axis=1)
def parts(t):
    return t.reshape(8, 16, -1, 4).transpose(0, 2, 1, 3)
def whole(p):
    return np.ascontiguousarray(p.transpose(0, 2, 1, 3)).reshape(128, -1)
def scan(p, key, start):
    h, o, g = np.array(start, np.float32), np.zeros((8, C, 16, 4), np.float32), np.arange(8)
    for j in range(C):
        n = np.maximum(np.float32(0.5) * h[g, key[:, j]], p[:, j])
        h[g, key[:, j]] = n
        o[:, j] = n
    return o, h
def same(a):
    return np.stack([a] * N)
def weights(rng, w):
    c, p = packed(same(w), rng)
    return {"wc": c, "ws": p}
def planted(rng, x, keys, size=np.ones((8, B)), swap=False, add=False, second=None):
    x[:, :, :8] = 0
    for e, k in ((0, keys),) if second is None else ((0, keys), (2, second)):
        for i in range(B):
            bit = k >> i & 1
            x[:, :, i, :, e] = (1 - bit).astype(np.float32).astype(BF)
            x[:, :, i, :, e + 1] = bit.astype(np.float32).astype(BF)
    u = np.zeros((128, 128, 4), np.float32)
    for g in range(8):
        for i in range(B):
            u[16 * g + i, 16 * g + i, 0] = size[g, i]
            u[16 * g + i, 16 * g + i, 1] = -size[g, i]
    w = np.zeros((128, 4, 128, 4), np.float32)
    i = np.arange(128)
    for b in range(4): w[i, b, i, b] = 32
    n = i[i % 16 < 8]
    turn = (1, 0, 2, 3) if swap else (0, 1, 2, 3) if second is None else (2, 3, 0, 1)
    for b in range(4):
        w[n, b, n, b] = 0
        w[n, b, n, turn[b]] = 32
    if add:
        n = i[(i % 16 >= 8) & (i % 16 < 12)]
        for b in range(4): w[n + 4, b, n, b] = 32
    return {"x": x.reshape(N, 128, 4 * C), "u": same(u.reshape(128, 512).astype(BF)), "v": same(np.array(f(rng, 128, 512))), **weights(rng, w.reshape(128, 2048).astype(BF))}
def numbers_of(rng):
    return np.array(f(rng, N, 128, 4 * C)).reshape(N, 8, 16, C, 4)
def three(rng, k, shape=(8, 4)):
    return rng.integers(4, 8, shape) * 2.0 ** k
def setup_inputs(rng):
    return {"x": np.array(f(rng, N, 128, 4 * C)), "u": same(np.array(f(rng, 128, 512))), "v": same(np.array(f(rng, 128, 512))), **weights(rng, np.array(f(rng, 128, 2048)))}
def setup_inputs_long(rng):
    r, j = np.arange(N)[:, None], np.arange(C)[None, :]
    a = rng.permutation(K)
    n = rng.integers(0, K, (N, C))
    third = 3 * rng.integers(0, K // 3, (N, C)) + (-r) % 3
    each = np.stack([rng.permutation(C) % K for i in range(N)])
    alone = np.where(j == rng.integers(0, 48, (N, 1)), 0, K - 1)
    p = [a[0], a[r + 1], a[N + 1 + r % 2], third, each, K - 1 - j * K // C, alone, np.where((r == 0) | (r == N - 1), n, a[N + 3])]
    keys = np.zeros((N, 8, C), int)
    heads = rng.permutation(8)
    for g, q in zip(heads, p): keys[:, g] = q
    first = keys.copy()
    x = numbers_of(rng)
    s = 65 + rng.integers(0, 2) - r * (80 // N)
    s[0] += 8
    for g, large in ((int(heads[0]), (C - 1 - j - s) % 80 == 0), (int(heads[6]), ((C - 1 - j) % 80 == 0) & (j >= 80))):
        first[:, g] = np.where(large, a[1], a[2])
        x[:, g, 8:, :, 2:] = three(rng, -30, (N, 8, C, 2)).astype(np.float32).astype(BF)
        x[:, g, 8:, :, :2] = np.where(large[:, None, :, None], three(rng, 27, (N, 8, C, 2)), 0.0).astype(np.float32).astype(BF)
        x[:, g, 8, :, 0] = np.where(large, 2.0 ** 30, 0.0).astype(np.float32).astype(BF)
    return planted(rng, x, first, second=keys)
def place_in_key(keys):
    o = np.argsort(keys, axis=-1, kind="stable")
    s = np.take_along_axis(keys, o, axis=-1)
    i = np.broadcast_to(np.arange(C), s.shape)
    head = np.ones(s.shape, bool)
    head[..., 1:] = s[..., 1:] != s[..., :-1]
    n = np.zeros(s.shape, int)
    np.put_along_axis(n, o, i - np.maximum.accumulate(np.where(head, i, 0), axis=-1), axis=-1)
    return n
def setup_inputs_near(rng):
    odd = rng.permutation(8) % 2
    size = np.exp2(np.where(odd, 28.0, -28.0))[:, None] * np.ones((8, B))
    low = rng.integers(0, B, 8)
    size[np.arange(8), low] = 0
    keys = rng.integers(0, K, (N, 8, C)) & ~(1 << low)[None, :, None]
    none = [rng.permutation(C)[:2] for r in range(N)]
    for r in range(N): keys[r][:, none[r]] = 0
    x = numbers_of(rng)
    m = (place_in_key(keys) % 2)[:, :, None, :, None]
    s = np.where(m == 0, 2.0, 1.0)
    up = (rng.integers(0, 2, (N, 8, 4, 1, 2)) + m) % 2
    x[:, :, 8:12, :, :2] = s.astype(np.float32).astype(BF)
    x[:, :, 12:, :, :2] = (s * (8 + up) * 2.0 ** -7).astype(np.float32).astype(BF)
    d = planted(rng, x, keys, size, add=True)
    x = d["x"].astype(np.float32).reshape(N, 8, 16, C, 4)
    for g in np.flatnonzero(odd == 0): x[:, g, :8] *= np.float32(2.0 ** -20)
    x = x.astype(BF).reshape(N, 128, C, 4)
    for r in range(N): x[r][:, none[r]] = 0
    return {**d, "x": x.reshape(N, 128, 4 * C)}
def setup_inputs_gone(rng):
    keys = 2 * rng.integers(0, K // 2, (N, 8, C)) + (np.arange(N)[:, None, None] + rng.integers(0, 2, (1, 8, 1))) % 2
    return planted(rng, numbers_of(rng), keys, swap=True)
def step(rng, v, n):
    return v * 2.0 ** -n + rng.choice([-1.0, 1.0], v.shape) * 2.0 ** (19 - n)
def runs(rng, t):
    v, s = three(rng, 20), [three(rng, -8) for i in range(4)]
    if t == 0: return [v] + s
    if t == 1: return s + [v]
    if t == 2: return [v, -2.0 * v] + s[:3]
    return [v] + [step(rng, v, n) for n in range(1, 5)]
def setup_inputs_order(rng):
    x = numbers_of(rng)
    keys = np.zeros((2, N, 8, C), int)
    def plant(r, g, j, k, v):
        keys[:, r, g, j] = k
        x[r, g, 8:, j] = v.astype(np.float32).astype(BF)
    firsts = rng.permutation(8) % (N - 3)
    for g in range(8):
        o = rng.permutation(K)
        keys[:, :, g] = o[9 + rng.integers(0, K - 9, (N, C))]
        at = [rng.permutation(C) for r in range(N)]
        for t in (0, 2):
            first = int(rng.integers(0, N - 1)) if g % 2 else 0
            v = three(rng, 20)
            plant(first, g, at[first][t], o[t], v)
            for r in range(first + 1, N): plant(r, g, at[r][t], o[t], three(rng, -8) if t == 0 else step(rng, v, r - first))
        a, b = 0, N - 1
        if g % 4:
            a = int(rng.integers(0, N - 2))
            b = int(rng.integers(a + 2, N))
        plant(a, g, at[a][1], o[1], three(rng, 20))
        plant(b, g, at[b][1], o[1], three(rng, -8))
        for t in range(4):
            for r in range(N):
                v = runs(rng, t)
                for i, j in enumerate(np.sort(at[r][3 + 5 * t:8 + 5 * t])): plant(r, g, j, o[3 + t], v[i])
        first = int(firsts[g])
        v = np.zeros((8, 4))
        v[7] = 11 * 2.0 ** (4 + rng.permutation([-1, 0, 0, 1]))
        plant(first, g, at[first][23], o[7], v)
        for r in range(first + 1, N):
            v = np.zeros((8, 4))
            v[:7] = three(rng, 20, (7, 4))
            plant(r, g, at[r][23], o[7], v)
            keys[0, r, g, at[r][23]] = o[8]
    return planted(rng, x, keys[0], second=keys[1])
def setup_inputs_spread(rng):
    d = setup_inputs(rng)
    x = wide(rng, N, 128, 4 * C).astype(np.float32) * np.repeat(np.exp2(rng.integers(-4, 5, (N, 1, C))), 4, axis=-1).astype(np.float32)
    d["x"] = np.array(mx_ref.flush(x.astype(BF)))
    return d
def check_inputs(d):
    b = []
    for k in ("x", "u", "v"):
        a = np.abs(d[k].astype(np.float32))
        if not (np.isfinite(a).all() and ((a == 0) | (a >= 2.0 ** -30) & (a <= 2.0 ** 30)).all()): b.append("a value of " + k)
    for k in ("u", "v"):
        a = d[k].astype(np.float32)
        if not (a == a[:1]).all(): b.append(k + " differs between ranks")
    if (d["wc"] != d["wc"][:1]).any(): b.append("wc differs between ranks")
    s = [mx_ref.live(p) for p in d["ws"]]
    if any((p != s[0]).any() for p in s): b.append("ws differs between ranks")
    if ((d["wc"] & 127) == 127).any(): b.append("a code of wc")
    a = np.max(np.abs(decode(pk(d["wc"][0], d["ws"][0]))).reshape(16, 8, -1, 4), axis=(1, 3))
    if not ((a == 0) | (a >= 2.0 ** -30) & (a <= 2.0 ** 30)).all(): b.append("a block of W")
    return b
def reference(x, u, v, wc, ws):
    w, qu, qv = pk(wc[0], ws[0]), mx_ref.quantize(u[0]), mx_ref.quantize(v[0])
    now = [mx_ref.quantize(x[r]) for r in range(N)]
    for t in range(R):
        p, key, last = [], [], []
        for r in range(N):
            key.append(key_of(mx_ref.matmul(qu, now[r])))
            made = tile([mx_ref.matmul(pick(w, np.arange(128 * b, 128 * b + 128)), now[r]) * np.float32(0.03125) for b in range(4)])
            p.append(parts(made.astype(np.float32)))
            h = scan(p[r], key[r], np.zeros((8, K, 16, 4), np.float32))[1]
            last.append(mx_ref.quantize(whole(h).astype(BF)))
        came = decode(join(*last))
        c, before = np.zeros((128, 4 * K), np.float32), []
        for r in range(N):
            before.append(mx_ref.quantize(c.astype(BF)))
            c = np.maximum(np.float32(0.5) * c, cut(came, r, 4 * K))
        start = decode(join(*before))
        for r in range(N):
            h = scan(p[r], key[r], parts(np.ascontiguousarray(cut(start, r, 4 * K))))[0]
            now[r] = mx_ref.quantize(whole(h).astype(BF))
    y = np.zeros((N, 128, C), np.float32)
    oc, osc = np.zeros((N, 128, 4 * C), np.uint8), np.zeros((N, 16, C), np.uint8)
    for r in range(N):
        y[r] = mx_ref.matmul(qv, now[r])
        oc[r], osc[r] = emit(now[r])
    return {"y": y, "oc": oc, "osc": osc}

@@ -1,0 +1,413 @@
+from concourse.bass import DstId, RemoteDMATransfer
+from concourse.mybir import dt, AluOpType, ActivationFunctionType
+
+C, K, R = 384, 32, 2
+L = C + K
+M = L + K
+NC = C // 16
+STEP = 1024.0
+TINY = 2.0 ** -126
+CODES, BF, F32 = "float8_e4m3fn_x4", "bfloat16", "float32"
+
+SCRATCH = {
+    "xb": ("sbuf", [128, 4 * C], BF), "ub": ("sbuf", [128, 4 * 144], BF), "vb": ("sbuf", [128, 512], BF),
+    "uq": ("sbuf", [128, 144], CODES), "us": ("sbuf", [128, 144], "uint8"),
+    "vq": ("sbuf", [128, 128], CODES), "vs": ("sbuf", [128, 128], "uint8"),
+    "wq": ("sbuf", [128, 512], CODES), "wp": ("sbuf", [128, 512], "uint8"),
+    "iq": ("sbuf", [128, 512], CODES), "ip": ("sbuf", [128, 512], "uint8"),
+    "lq": ("sbuf", [128, 320], CODES), "lp": ("sbuf", [128, 320], "uint8"),
+    "cq": ("sbuf", [128, 128], CODES), "cp": ("sbuf", [128, 128], "uint8"),
+    "pi": ("sbuf", [128, 4], "int32"), "cf": ("sbuf", [128, 8], F32), "acc": ("sbuf", [128, 2], F32),
+    "mv": ("sbuf", [128, 64], BF), "s16": ("sbuf", [128, L], BF), "dm": ("sbuf", [128, L], BF),
+    "jv": ("sbuf", [128, L], F32), "one": ("sbuf", [128, 516], BF), "z32": ("sbuf", [128, 32], BF),
+    "b2": ("sbuf", [128, NC, 2, 16], BF), "bt": ("sbuf", [128, NC, 32], BF),
+    "b5": ("sbuf", [128, 5 * NC], BF), "hn": ("sbuf", [128, 5 * NC], BF), "ky": ("sbuf", [128, 5 * NC], BF),
+    "zz": ("sbuf", [128, 32 * NC], BF), "dn": ("sbuf", [128, C], BF),
+    "mt": ("sbuf", [128, 2 * M], BF), "mk": ("sbuf", [128, NC + 2, 2, 16], BF),
+    "xe": ("sbuf", [128, 2 * M], BF), "sg": ("sbuf", [128, 2 * C], BF), "cu": ("sbuf", [128, 2 * M], BF),
+    "st": ("sbuf", [128, NC + 4, 2, 16], BF), "stt": ("sbuf", [128, 2 * M], BF), "sel": ("sbuf", [128, 2 * M], BF),
+    "pl": ("sbuf", [128, NC + 4], "uint16"), "il": ("sbuf", [128, NC + 2], "uint16"),
+    "inv": ("sbuf", [128, L], F32), "dg": ("sbuf", [128, L], F32),
+    "h0": ("sbuf", [128, L], BF), "h1": ("sbuf", [128, L], BF),
+    "pw": ("sbuf", [128, 4 * L], BF), "pz": ("sbuf", [128, 4 * L], BF), "hs": ("sbuf", [128, 4 * L], BF),
+    "et": ("sbuf", [128, 512], BF), "ct": ("sbuf", [128, 512], BF), "ht": ("sbuf", [128, 4 * C], BF),
+    "cm": ("sbuf", [128, 96], BF), "dd": ("sbuf", [128, 384], BF), "d2": ("sbuf", [128, 128], BF), "cc": ("sbuf", [128, 128], BF),
+    "yb": ("sbuf", [128, C], F32),
+}
+for _t in range(R + 1):
+    SCRATCH["aq%d" % _t] = ("sbuf", [128, C], CODES)
+    SCRATCH["ap%d" % _t] = ("sbuf", [128, C], "uint8")
+for _t in range(R):
+    SCRATCH["eq%d" % _t] = ("sbuf", [128, 128], CODES)
+    SCRATCH["ep%d" % _t] = ("sbuf", [128, 128], "uint8")
+for _t in range(8):
+    SCRATCH["ps%d" % _t] = ("psum", [128, 512], F32)
+
+SEMAPHORES = ["cv", "cs", "ct", "cg", "lu", "lu2", "lx", "lx2", "lw", "lp", "lv", "oy", "oc", "sent", "arr0", "arr1"]
+
+
+def plan_calls(topo, cores, r):
+    src = cores[r]
+    later = list(range(r + 1, len(cores)))
+    if not later:
+        return []
+    width = min(len(topo.engines(src, cores[d])) for d in range(len(cores)) if d != r)
+    calls = []
+    for d in later:
+        can = topo.engines(src, cores[d])
+        for call in calls:
+            used = [e for _, es in call for e in es]
+            free = [e for e in can if e not in used]
+            if len(free) >= width:
+                call.append((d, free[-width:]))
+                break
+        else:
+            calls.append([(d, can[-width:])])
+    return calls
+
+
+def emit(g, T, ops):
+    queue = {"v": g.vector, "s": g.scalar, "t": g.tensor, "g": g, "y": g.sync}
+    writer, readers, deps = {}, {}, []
+    for i, o in enumerate(ops):
+        d = set()
+        for k in o["r"]:
+            if k in writer: d.add(writer[k])
+        for k in o["w"]:
+            if k in writer: d.add(writer[k])
+            d.update(readers.get(k, []))
+        for k in o["r"]:
+            readers.setdefault(k, []).append(i)
+        for k in o["w"]:
+            writer[k] = i
+            readers[k] = []
+        d.discard(i)
+        deps.append(d)
+    needed = set()
+    for d in deps: needed.update(d)
+    count, mark, know, clock = {}, {}, {}, {q: {} for q in queue}
+    for i, o in enumerate(ops):
+        q = o["q"]
+        if q is None:
+            mark[i], know[i] = (o["sem"], o["n"]), {o["sem"]: o["n"]}
+            continue
+        want = {}
+        for j in deps[i]:
+            s, n = mark[j]
+            if want.get(s, (0, 0))[0] < n: want[s] = (n, j)
+        for s, (n, j) in sorted(want.items(), key=lambda e: -e[1][1]):
+            if clock[q].get(s, 0) < n:
+                queue[q].wait_ge(T.sem[s], n)
+                for s2, n2 in know[j].items():
+                    if clock[q].get(s2, 0) < n2: clock[q][s2] = n2
+        ins = o["f"]()
+        s, n = (o["sem"], 16) if o["sem"] else ("c" + q, 1)
+        if ins is not None and (o["sem"] or i in needed):
+            ins.then_inc(T.sem[s], n)
+            count[s] = count.get(s, 0) + n
+            mark[i] = (s, count[s])
+            know[i] = dict(clock[q])
+            know[i][s] = count[s]
+
+
+def rank_program(g, core, T, topo):
+    rank = T.rank_of(core)
+    if rank is None:
+        return
+    cores = list(T.cores)
+    n_ranks = len(cores)
+    A, ACT = AluOpType, ActivationFunctionType
+    ops = []
+
+    def op(q, f, r=(), w=(), sem=None, n=0):
+        ops.append({"q": q, "f": f, "r": list(r), "w": list(w), "sem": sem, "n": n})
+
+    def ts(out, in0, s1, s2, op0, op1, r, w):
+        if s2 is None: op("v", lambda: g.vector.tensor_scalar(out, in0, s1, None, op0), r, w)
+        else: op("v", lambda: g.vector.tensor_scalar(out, in0, s1, s2, op0, op1), r, w)
+
+    def fill(out, c, w):
+        op("v", lambda: g.vector.memset(out, c), (), w)
+
+    def count_up(out, pattern, base, cm, w):
+        op("g", lambda: g.iota(out, pattern, base, cm, allow_small_or_imprecise_dtypes=True), (), w)
+
+    def turn(out, in_, r, w):
+        op("v", lambda: g.vector.transpose(out, in_), r, w)
+
+    def scan(out, d0, d1, init, op0, op1, r, w):
+        op("v", lambda: g.vector.tensor_tensor_scan(out, d0, d1, init, op0, op1), r, w)
+
+    def move(q, out, in_, r, w):
+        if q == "v": op("v", lambda: g.vector.tensor_copy(out, in_), r, w)
+        else: op("s", lambda: g.scalar.activation(out, in_, ACT.Copy), r, w)
+
+    def quant(codes, plane, in_, r, w):
+        op("v", lambda: g.vector.quantize_mx(codes, plane, in_), r, w)
+
+    def product(out, lq, lp, rq, rp, r, w):
+        op("t", lambda: g.tensor.matmul_mx(out, lq, lp, rq, rp, True, True), r, w)
+
+    def dma(q, out, in_, sem, r, w):
+        e = g.sync if q == "y" else g.scalar
+        op(q, lambda: e.dma_start(out, in_), r, w, sem)
+
+    ps = [T["ps%d" % b] for b in range(8)]
+    col = lambda i: T.cf[:, i:i + 1]
+    OD, XK, XF, XO, KK = range(5)
+    sends = rank < n_ranks - 1
+    hc, hn = C // 2, NC // 2
+
+    dma("y", T.ub[:, 0:512], T.u[:], "lu", [], ["ub0"])
+    dma("s", T.ub[:, 512:576], T.u[:, 0:64], "lu2", [], ["ub1"])
+    dma("y", T.xb[:, 0:4 * hc], T.x[:, 0:4 * hc], "lx", [], ["xb0"])
+    dma("y", T.xb[:, 4 * hc:4 * C], T.x[:, 4 * hc:4 * C], "lx2", [], ["xb1"])
+    dma("y", T.wq[:].bitcast(dt.uint8), T.wc[:], "lw", [], ["wq"])
+    dma("y", T.wp[:], T.ws[:], "lp", [], ["wp"])
+    dma("y", T.vb[:], T.v[:], "lv", [], ["vb"])
+
+    op("g", lambda: g.iota(T.pi[:, 0:1], [[0, 1]], 0, 1), (), ["pi0"])
+    count_up(T.mv[:], [[16 * int(STEP), 2], [-int(STEP), 32]], int(STEP), 0, ["mv"])
+    count_up(T.s16[:], [[0, NC + 2], [1, 16]], 0, 0, ["s16"])
+    count_up(T.jv[:], [[1, L]], 0, 0, ["jv"])
+    count_up(T.z32[:], [[0, 32]], 0, 0, ["z32"])
+    for b in range(4):
+        count_up(T.pw[:, L * b:L * b + K], [[0, K]], 0, 0, ["pw0%d" % b])
+    if sends:
+        count_up(T.et[:, 128:512], [[0, 384]], 0, 0, ["et0"])
+    if rank > 0:
+        count_up(T.one[:], [[0, 516]], 1, 0, ["one"])
+        op("g", lambda: g.affine_select(T.one[:], T.one[:], [[-1, 516]], A.is_equal, 0.0, 3, 4), ["one"], ["one"])
+
+    fill(T.hn[:], 0.5, ["hn"])
+    fill(T.dn[:], -STEP, ["dn"])
+    fill(T.zz[:], 0.0, ["zz"])
+    ts(T.pi[:, 1:2], T.pi[:, 0:1], 16, None, A.bitwise_and, None, ["pi0"], ["pi1"])
+    ts(T.pi[:, 2:3], T.pi[:, 0:1], 15, None, A.bitwise_and, None, ["pi0"], ["pi2"])
+    ts(T.pi[:, 3:4], T.pi[:, 0:1], 31, None, A.bitwise_and, None, ["pi0"], ["pi3"])
+    fill(T.hn[:, 0::5], 0.0, ["hn"])
+    fill(T.h0[:], 0.5, ["h0"])
+    odd, lane = T.pi[:, 1:2], T.pi[:, 2:3]
+    ts(col(OD), odd, 15.5 * STEP / 16, STEP, A.mult, A.add, ["pi1"], ["od"])
+    ts(col(XK), lane, STEP, None, A.mult, None, ["pi2"], ["xk"])
+    ts(col(XF), lane, 1.0, None, A.mult, None, ["pi2"], ["xf"])
+    ts(col(XO), lane, -512.0, 7680.0, A.mult, A.add, ["pi2"], ["xo"])
+    ts(col(KK), T.pi[:, 3:4], 2.0, float(C), A.mult, A.add, ["pi3"], ["kk"])
+    for h in range(2):
+        fill(T.xe[:, M * h + L:M * h + M], 0.0, ["xe2%d" % h])
+    ts(T.mt[:, 0:64], T.mv[:], col(XK), 0.0, A.add, A.max, ["mv", "xk"], ["mt0"])
+    ts(T.mt[:, 2 * L:2 * M], T.mv[:], col(XK), 0.0, A.add, A.max, ["mv", "xk"], ["mt2"])
+    turn(T.mk[:, 0:2], T.mt[:, 0:64], ["mt0"], ["mk0"])
+    ts(T.dm[:], T.s16[:], col(XF), -16384.0, A.is_equal, A.mult, ["s16", "xf"], ["dm"])
+    for h in range(2):
+        ts(T.xe[:, M * h:M * h + K], T.mk[:, 0:2, h, :], STEP, None, A.is_equal, None, ["mk0"], ["xe0%d" % h])
+    ts(T.dm[:], T.dm[:], 512.0, None, A.add, None, ["dm"], ["dm"])
+    quant(T.uq[:], T.us[:], T.ub[:], ["ub0", "ub1"], ["uq"])
+
+    def state(t, h, tile, r):
+        c = slice(hc * h, hc * h + hc)
+        quant(T["aq%d" % t][:, c], T["ap%d" % t][:, c], tile[:, 4 * hc * h:4 * hc * h + 4 * hc], r, ["a%d%d" % (t, h)])
+
+    calls = plan_calls(topo, cores, rank)
+    sent = [0]
+
+    def landing(t, d, s):
+        return (96 - K * d if t == 0 else 224) + K * s
+
+    def send(t):
+        order = calls
+        if t < R - 1:
+            order = [[e for e in call if (e[0] == n_ranks - 1) == late] for late in (False, True) for call in calls]
+        for call in [c for c in order if c]:
+            for part in range(2):
+                def issue(call=call, part=part):
+                    tr = []
+                    for d, es in call:
+                        a = landing(t, d, rank)
+                        rid, pid = topo.addr(cores[d])[0:2]
+                        if part == 0:
+                            src, dst = T["eq%d" % t][:, 0:K].bitcast(dt.uint8), T.lq[:, a:a + K].bitcast(dt.uint8)
+                        else:
+                            src, dst = T["ep%d" % t][:, 0:K], T.lp[:, a:a + K]
+                        tr.append(RemoteDMATransfer(dst_ids=[DstId(rid=rid, pnc=pid)], dma_engine_mask=sum(1 << e for e in es),
+                                                    remote_sem=T.sem["arr%d" % t], src=src, dst=dst))
+                        sent[0] += len(es)
+                    g.remote_dma_fused(tr, local_sem=T.sem.sent)
+                op("g", issue, ["e%d" % t], [])
+
+    arriving = 2 * sum(len(es) for s in range(rank) for call in plan_calls(topo, cores, s) for d, es in call if d == rank)
+    slots, ends = T.pl[:, 0:2], T.pl[:, NC + 2:NC + 4]
+    plane = lambda buf, b: buf[:, L * b:L * b + L]
+
+    def one_round(t):
+        aq, ap, a = T["aq%d" % t], T["ap%d" % t], ["a%d0" % t, "a%d1" % t]
+        half, hk = T["h%d" % t], "h%d" % t
+
+        def signs(h):
+            c, k = slice(hc * h, hc * h + hc), slice(hn * h, hn * h + hn)
+            for o in (1, 0):
+                product(ps[2 * h + o][:, 0:hc], T.uq[:, 16 * o:16 * o + 128], T.us[:, 16 * o:16 * o + 128], aq[:, c], ap[:, c],
+                        ["uq", a[h]], ["ps%d" % (2 * h + o)])
+            ts(T.b2[:, k, 0, :], ps[2 * h][:, 0:hc], 0.0, 2.0, A.is_lt, A.mult, [], ["ps%d" % (2 * h), "b20%d" % h])
+            op("s", lambda: g.scalar.activation(T.b2[:, k, 1, :], ps[2 * h + 1][:, 0:hc], ACT.Sign, -TINY, -1.0),
+               [], ["ps%d" % (2 * h + 1), "b21%d" % h])
+
+        def bits(h):
+            k = slice(hn * h, hn * h + hn)
+            turn(T.bt[:, k], T.b2[:, k], ["b20%d" % h, "b21%d" % h], ["bt%d" % h])
+
+        def five(h):
+            move("v", T.b5[:, 5 * hn * h:5 * hn * (h + 1)], T.bt[:, hn * h:hn * h + hn, 0:5], ["bt%d" % h], ["b5%d" % h])
+
+        def key(h):
+            c = slice(5 * hn * h, 5 * hn * (h + 1))
+            scan(T.ky[:, c], T.hn[:, c], T.b5[:, c], 0.0, A.mult, A.add, ["hn", "b5%d" % h], ["ky%d" % h])
+
+        def head(h):
+            ts(T.zz[:, C * h:C * h + C:32], T.ky[:, 5 * hn * h + 4:5 * hn * (h + 1):5], 8 * STEP, col(OD), A.mult, A.add,
+               ["ky%d" % h, "od", "zz"], ["zz%d" % h])
+
+        def down(h):
+            scan(T.mt[:, 64 + C * h:64 + C * h + C], T.dn[:], T.zz[:, C * h:C * h + C], 0.0, A.add, A.max,
+                 ["dn", "zz", "zz%d" % h], ["mt1%d" % h])
+
+        def by_key(h):
+            turn(T.mk[:, 2 + hn * h:2 + hn * h + hn], T.mt[:, 64 + C * h:64 + C * h + C], ["mt1%d" % h], ["mk1%d" % h])
+
+        def own(o, h):
+            ts(T.xe[:, M * o + K + hc * h:M * o + K + hc * h + hc], T.mk[:, 2 + hn * h:2 + hn * h + hn, o, :], STEP, None, A.is_equal, None,
+               ["mk1%d" % h], ["xe1%d%d" % (o, h)])
+
+        if t == 0: state(0, 0, T.xb, ["xb0"])
+        signs(0)
+        if t == 0: state(0, 1, T.xb, ["xb1"])
+        bits(0); signs(1)
+        for b in range(4):
+            product(ps[4 + b][:, 0:C], T.wq[:, 128 * b:128 * b + 128], T.wp[:, 128 * b:128 * b + 128], aq[:], ap[:],
+                    ["wq", "wp"] + a, ["ps%d" % (4 + b)])
+        five(0); bits(1); key(0); five(1); head(0); key(1); down(0); head(1); by_key(0); down(1)
+        own(0, 0); by_key(1); own(1, 0); own(0, 1); own(1, 1)
+        for o in range(2):
+            op("s", lambda o=o: g.scalar.activation(T.sg[:, C * o:C * o + C], T.mk[:, 2:NC + 2, o, :], ACT.Sign, 512.0, -1.0,
+                                                    accum_out=T.acc[:, o:o + 1]), ["mk10", "mk11"], ["sg%d" % o, "acc%d" % o])
+        for b in range(4):
+            op("s", lambda b=b: g.scalar.activation(T.pw[:, L * b + K:L * b + L], ps[4 + b][:, 0:C], ACT.Copy, 0.0, 0.03125),
+               [], ["ps%d" % (4 + b), "pw1%d" % b])
+        for o in range(2):
+            xe = T.xe[:, M * o:M * o + M]
+            scan(T.cu[:, M * o:M * o + M], xe, xe, -float(L), A.add, A.add,
+                 ["xe0%d" % o, "xe1%d0" % o, "xe1%d1" % o, "xe2%d" % o], ["cu%d" % o])
+        hm, hs = M // 2, hn + 2
+        for o in range(2):
+            for h in range(2):
+                ts(T.st[:, hs * h:hs * h + hs, o, :], T.cu[:, M * o + hm * h:M * o + hm * h + hm], T.acc[:, o:o + 1], col(KK), A.add, A.add,
+                   ["kk", "cu%d" % o, "acc%d" % o], ["st%d%d" % (o, h)])
+        for h in range(2):
+            turn(T.stt[:, M * h:M * h + M], T.st[:, hs * h:hs * h + hs], ["st0%d" % h, "st1%d" % h], ["stt%d" % h])
+        for h in range(2):
+            scan(T.sel[:, M * h:M * h + M], T.mt[:, M * h:M * h + M], T.stt[:, M * h:M * h + M], 0.0, A.add, A.min,
+                 ["mt0", "mt1%d" % h, "mt2", "stt%d" % h], ["sel%d" % h])
+        ts(T.pl[:], T.sel[:, 31::32], 0.5, L / 2 - 1.0, A.mult, A.add, ["sel0", "sel1"], ["pl"])
+        move("v", T.inv[:].indirect(T.pl[:, 0:NC + 2]), T.jv[:], ["pl", "jv"], ["inv"])
+        scan(T.dg[:], T.dm[:], T.inv[:], 0.0, A.add, A.max, ["dm", "inv"], ["dg"])
+        ts(T.il[:], T.dg[:, 15::16], col(XO), None, A.subtract, None, ["dg", "xo"], ["il"])
+        move("v", half[:].indirect(slots), T.z32[:], ["pl", "z32"], [hk])
+
+        def sort(q, b, c0=0, c1=NC + 2, tag=""):
+            w = ["pz%d%s" % (b, x) for x in (tag or "ab")]
+            move(q, T.pz[:, L * b + 16 * c0:L * b + 16 * c1], plane(T.pw, b).indirect(T.il[:, c0:c1]),
+                 ["il", "pw0%d" % b, "pw1%d" % b], w)
+
+        def run(b):
+            scan(plane(T.hs, b), half[:], plane(T.pz, b), 0.0, A.mult, A.max, [hk, "pz%da" % b, "pz%db" % b], ["hs%d" % b])
+
+        def last(q, b):
+            move(q, T.et[:, b:128:4], plane(T.hs, b).indirect(ends), ["pl", "hs%d" % b], ["et1%d" % b])
+
+        def unsort(q, b, h0=0, h1=2):
+            move(q, T.ht[:, 4 * hc * h0 + b:4 * hc * h1:4], plane(T.hs, b).indirect(T.pl[:, 2 + hn * h0:2 + hn * h1]),
+                 ["pl", "hs%d" % b], ["ht%d%d" % (b, h) for h in range(h0, h1)])
+
+        def new_state():
+            unsort("s", 0); unsort("s", 1, 0, 1); unsort("v", 2, 0, 1); unsort("s", 3, 0, 1)
+            state(t + 1, 0, T.ht, ["ht%d0" % b for b in range(4)])
+            unsort("s", 1, 1, 2); unsort("v", 2, 1, 2); unsort("s", 3, 1, 2)
+            state(t + 1, 1, T.ht, ["ht%d1" % b for b in range(4)])
+
+        if sends:
+            sort("s", 0); sort("v", 2); sort("s", 1)
+            sort("v", 3, 0, 14, "a"); sort("s", 3, 14, NC + 2, "b")
+            run(2); run(0); run(1); run(3)
+            last("s", 2); last("s", 0); last("s", 1); last("v", 3)
+            quant(T["eq%d" % t][:], T["ep%d" % t][:], T.et[:], ["et0"] + ["et1%d" % b for b in range(4)], ["e%d" % t])
+            send(t)
+        else:
+            sort("s", 0); sort("v", 2); sort("s", 1); sort("v", 3)
+
+        if rank == 0:
+            new_state()
+        if t == 0:
+            if rank > 0:
+                fill(T.ct[:], 0.0, ["ct"])
+                for b in range(4):
+                    quant(T.iq[:, 128 * b:128 * b + 128], T.ip[:, 128 * b:128 * b + 128], T.one[:, 3 - b:515 - b], ["one"], ["i%d" % b])
+                quant(T.lq[:, 96:224], T.lp[:, 96:224], T.ct[:], ["ct"], ["lz"])
+                if rank > 1:
+                    for s in range(rank):
+                        fill(T.cm[:, K * s:K * s + K], 0.5 ** (rank - 1 - s), ["cm%d" % s])
+            fill(T.h1[:], 0.5, ["h1"])
+            quant(T.vq[:], T.vs[:], T.vb[:], ["vb"], ["vq"])
+        if rank > 0:
+            op(None, None, [], ["land%d" % t], "arr%d" % t, arriving)
+            v0 = 96 - K * rank if t == 0 else 96 + K * rank
+            e0 = landing(t, rank, 0) - v0
+            n = K * rank
+            for b in range(4):
+                product(ps[b][:, 0:128], T.iq[:, 128 * b:128 * b + 128], T.ip[:, 128 * b:128 * b + 128],
+                        T.lq[:, v0:v0 + 128], T.lp[:, v0:v0 + 128], ["i%d" % b, "lz", "land%d" % t], ["ps%d" % b])
+            if rank == 1:
+                for b in range(4):
+                    move("sv"[b % 2], T.ct[:, b:128:4], ps[b][:, e0:e0 + K], ["ct"], ["ps%d" % b, "ct%d" % b])
+                made = ["ct%d" % b for b in range(4)]
+            else:
+                for b in range(4):
+                    op("v", lambda b=b: g.vector.tensor_tensor(T.dd[:, b:4 * n:4], ps[b][:, e0:e0 + n], T.cm[:, 0:n], A.mult),
+                       ["cm%d" % s for s in range(rank)], ["ps%d" % b, "dd%d" % b])
+                dd = ["dd%d" % b for b in range(4)]
+                prev, pk = T.dd[:, 0:128], []
+                for s in range(1, rank):
+                    out, ok = (T.ct[:, 0:128], "ct0") if s == rank - 1 else (T.d2[:], "d2")
+                    op("v", lambda out=out, prev=prev, s=s: g.vector.tensor_tensor(out, prev, T.dd[:, 128 * s:128 * s + 128], A.max),
+                       dd + pk + ["ct"], [ok])
+                    prev, pk = out, [ok]
+                made = ["ct0"]
+            quant(T.cq[:], T.cp[:], T.ct[:], ["ct"] + made, ["cq"])
+            for b in range(4):
+                product(ps[4 + b][:, 0:128], T.iq[:, 128 * b:128 * b + 128], T.ip[:, 128 * b:128 * b + 128],
+                        T.cq[:], T.cp[:], ["i%d" % b, "cq"], ["ps%d" % (4 + b)])
+            for b in range(4):
+                move("s", T.cc[:, K * b:K * b + K], ps[4 + b][:, 0:K], [], ["ps%d" % (4 + b), "cc%d" % b])
+            for b in range(5):
+                if b < 4:
+                    move("v", plane(T.pz, b).indirect(slots), T.cc[:, K * b:K * b + K], ["pl", "cc%d" % b], ["pz%da" % b, "pz%db" % b])
+                if b > 0: run(b - 1)
+            new_state()
+
+    for t in range(R):
+        one_round(t)
+
+    aq, ap, a = T["aq%d" % R], T["ap%d" % R], ["a%d0" % R, "a%d1" % R]
+    for h in range(2):
+        c = slice(hc * h, hc * h + hc)
+        product(ps[h][:, 0:hc], T.vq[:], T.vs[:], aq[:, c], ap[:, c], ["vq", a[h]], ["ps%d" % h])
+        dma("y", T.oc[:, 4 * hc * h:4 * hc * h + 4 * hc], aq[:, c].bitcast(dt.uint8), "oc", [a[h]], [])
+        move("s", T.yb[:, c], ps[h][:, 0:hc], [], ["ps%d" % h, "y%d" % h])
+        dma("s", T.y[:, c], T.yb[:, c], "oy", ["y%d" % h], [])
+    for k in range(4):
+        dma("y", T.osc[4 * k:4 * k + 4, :], ap[32 * k:32 * k + 4, :], "oc", a, [])
+
+    emit(g, T, ops)
+    g.sync.wait_ge(T.sem.oc, 16 * 6)
+    g.scalar.wait_ge(T.sem.oy, 16 * 2)
+    if sent[0]:
+        g.wait_ge(T.sem.sent, sent[0])

@@ -4,46 +4,49 @@ from concourse.mybir import dt, AluOpType, ActivationFunctionType
 C, K, R = 384, 32, 2
 L = C + K
 M = L + K
-NC = C // 16
-STEP = 1024.0
+X = M + K
+W = C + 16
+UNIT = 2.0 ** -10
+LIFT = 2.0 ** 14
 TINY = 2.0 ** -126
-CODES, BF, F32 = "float8_e4m3fn_x4", "bfloat16", "float32"
+CODES, BF, F32, U16 = "float8_e4m3fn_x4", "bfloat16", "float32", "uint16"
+
+PIECES = [((0, c), (c, C)) for c in (192, 224, 192)]
+SORT = ((0, "s", 0, 26), (2, "v", 0, 26), (1, "s", 0, 26), (3, "v", 0, 18), (3, "s", 18, 26))
+UNSORT = [("sssv", "ssvv"), ("ssvv", "sssv")]
+WAIT = 250
+CYCLE = 0.83
+AHEAD = {"tb": 300, "sel2": 600}
 
 SCRATCH = {
-    "xb": ("sbuf", [128, 4 * C], BF), "ub": ("sbuf", [128, 4 * 144], BF), "vb": ("sbuf", [128, 512], BF),
-    "uq": ("sbuf", [128, 144], CODES), "us": ("sbuf", [128, 144], "uint8"),
-    "vq": ("sbuf", [128, 128], CODES), "vs": ("sbuf", [128, 128], "uint8"),
-    "wq": ("sbuf", [128, 512], CODES), "wp": ("sbuf", [128, 512], "uint8"),
-    "iq": ("sbuf", [128, 512], CODES), "ip": ("sbuf", [128, 512], "uint8"),
-    "lq": ("sbuf", [128, 320], CODES), "lp": ("sbuf", [128, 320], "uint8"),
-    "cq": ("sbuf", [128, 128], CODES), "cp": ("sbuf", [128, 128], "uint8"),
-    "pi": ("sbuf", [128, 4], "int32"), "cf": ("sbuf", [128, 8], F32), "acc": ("sbuf", [128, 2], F32),
-    "mv": ("sbuf", [128, 64], BF), "s16": ("sbuf", [128, L], BF), "dm": ("sbuf", [128, L], BF),
-    "jv": ("sbuf", [128, L], F32), "one": ("sbuf", [128, 516], BF), "z32": ("sbuf", [128, 32], BF),
-    "b2": ("sbuf", [128, NC, 2, 16], BF), "bt": ("sbuf", [128, NC, 32], BF),
-    "b5": ("sbuf", [128, 5 * NC], BF), "hn": ("sbuf", [128, 5 * NC], BF), "ky": ("sbuf", [128, 5 * NC], BF),
-    "zz": ("sbuf", [128, 32 * NC], BF), "dn": ("sbuf", [128, C], BF),
-    "mt": ("sbuf", [128, 2 * M], BF), "mk": ("sbuf", [128, NC + 2, 2, 16], BF),
-    "xe": ("sbuf", [128, 2 * M], BF), "sg": ("sbuf", [128, 2 * C], BF), "cu": ("sbuf", [128, 2 * M], BF),
-    "st": ("sbuf", [128, NC + 4, 2, 16], BF), "stt": ("sbuf", [128, 2 * M], BF), "sel": ("sbuf", [128, 2 * M], BF),
-    "pl": ("sbuf", [128, NC + 4], "uint16"), "il": ("sbuf", [128, NC + 2], "uint16"),
-    "inv": ("sbuf", [128, L], F32), "dg": ("sbuf", [128, L], F32),
-    "h0": ("sbuf", [128, L], BF), "h1": ("sbuf", [128, L], BF),
-    "pw": ("sbuf", [128, 4 * L], BF), "pz": ("sbuf", [128, 4 * L], BF), "hs": ("sbuf", [128, 4 * L], BF),
+    "xb": ("sbuf", [128, 4 * C], BF), "ub": ("sbuf", [128, 512], BF), "vb": ("sbuf", [128, 512], BF),
+    "pi": ("sbuf", [128, 10], "int32"), "cf": ("sbuf", [128, 16], F32), "acc": ("sbuf", [128, 4], F32),
+    "ui": ("sbuf", [128, 8], F32), "ul": ("sbuf", [128, 8], U16), "zi": ("sbuf", [128, 2], F32), "zl": ("sbuf", [128, 6], U16),
+    "mv": ("sbuf", [128, 64], BF), "s16": ("sbuf", [128, 48], BF), "dm": ("sbuf", [128, L], BF), "dl": ("sbuf", [128, 26], U16),
+    "ji": ("sbuf", [128, C // 2], BF), "jv": ("sbuf", [128, C], BF),
+    "one": ("sbuf", [128, 516], BF), "z32": ("sbuf", [128, 32], BF), "on": ("sbuf", [128, X], BF),
+    "b2": ("sbuf", [128, C], BF), "bt": ("sbuf", [128, L], BF), "hn": ("sbuf", [128, 64], BF),
+    "zz": ("sbuf", [128, 2 * M], BF), "dn": ("sbuf", [128, 256], BF),
+    "mt": ("sbuf", [128, 2 * M], BF), "mk": ("sbuf", [128, 2 * C], BF), "sg": ("sbuf", [128, 2 * C], BF),
+    "xe": ("sbuf", [128, 2 * X], BF), "cu": ("sbuf", [128, 2 * X], BF), "st": ("sbuf", [128, 2 * M], BF),
+    "sel": ("sbuf", [128, 64 + 1056], BF), "tb": ("sbuf", [128, 64], BF),
+    "pl": ("sbuf", [128, 32], U16), "pa": ("sbuf", [128, 32], U16), "il": ("sbuf", [128, 26], U16), "dg": ("sbuf", [128, L], BF),
+    "pw": ("sbuf", [128, 4 * W], BF), "pz": ("sbuf", [128, 4 * L], BF), "hs": ("sbuf", [128, 4 * L], BF),
     "et": ("sbuf", [128, 512], BF), "ct": ("sbuf", [128, 512], BF), "ht": ("sbuf", [128, 4 * C], BF),
-    "cm": ("sbuf", [128, 96], BF), "dd": ("sbuf", [128, 384], BF), "d2": ("sbuf", [128, 128], BF), "cc": ("sbuf", [128, 128], BF),
+    "cm": ("sbuf", [128, 64], BF), "dd": ("sbuf", [128, 256], BF), "d2": ("sbuf", [128, 128], BF), "cc": ("sbuf", [128, 128], BF),
     "yb": ("sbuf", [128, C], F32),
 }
-for _t in range(R + 1):
-    SCRATCH["aq%d" % _t] = ("sbuf", [128, C], CODES)
-    SCRATCH["ap%d" % _t] = ("sbuf", [128, C], "uint8")
+for _n, _w in (("t", 128), ("u", 128), ("v", 128), ("w", 512), ("i", 512), ("l", 320), ("c", 128),
+               ("a0", C), ("a1", C), ("a2", C), ("e0", 128), ("e1", 128)):
+    SCRATCH[_n + "q"] = ("sbuf", [128, _w], CODES)
+    SCRATCH[_n + "p"] = ("sbuf", [128, _w], "uint8")
 for _t in range(R):
-    SCRATCH["eq%d" % _t] = ("sbuf", [128, 128], CODES)
-    SCRATCH["ep%d" % _t] = ("sbuf", [128, 128], "uint8")
+    SCRATCH["h%d" % _t] = ("sbuf", [128, L], BF)
+    SCRATCH["inv%d" % _t] = ("sbuf", [128, L], BF)
 for _t in range(8):
     SCRATCH["ps%d" % _t] = ("psum", [128, 512], F32)
 
-SEMAPHORES = ["cv", "cs", "ct", "cg", "lu", "lu2", "lx", "lx2", "lw", "lp", "lv", "oy", "oc", "sent", "arr0", "arr1"]
+SEMAPHORES = ["cv", "cs", "ct", "cg", "lu", "lx", "lx2", "lw", "lp", "lv", "oy", "oc", "sent", "arr0", "arr1", "arr2"]
 
 
 def plan_calls(topo, cores, r):
@@ -66,36 +69,70 @@ def plan_calls(topo, cores, r):
     return calls
 
 
-def emit(g, T, ops):
-    queue = {"v": g.vector, "s": g.scalar, "t": g.tensor, "g": g, "y": g.sync}
-    writer, readers, deps = {}, {}, []
+def needs(ops):
+    writers, readers, waits, after = {}, {}, [], []
     for i, o in enumerate(ops):
-        d = set()
+        d, a = set(), set()
         for k in o["r"]:
-            if k in writer: d.add(writer[k])
+            d.update(writers.get(k, []))
         for k in o["w"]:
-            if k in writer: d.add(writer[k])
-            d.update(readers.get(k, []))
+            for j in writers.get(k, []) + readers.get(k, []):
+                (a if ops[j]["q"] == o["q"] and (k == "calls" or k[:2] == "ps" and o["q"] != "t") else d).add(j)
         for k in o["r"]:
             readers.setdefault(k, []).append(i)
         for k in o["w"]:
-            writer[k] = i
+            writers[k] = [j for j in writers.get(k, []) if j in a] + [i]
             readers[k] = []
-        d.discard(i)
-        deps.append(d)
+        waits.append(d - {i})
+        after.append(a - d - {i})
+    return waits, after
+
+
+def arrange(ops, waits, after):
+    n = len(ops)
+    way = [o["ns"] + o["on"] for o in ops]
+    for i in range(n - 1, -1, -1):
+        for j in waits[i]: way[j] = max(way[j], ops[j]["ns"] + WAIT + way[i])
+        for j in after[i]: way[j] = max(way[j], ops[j]["ns"] + way[i])
+    way = [way[i] + AHEAD.get((ops[i]["w"] or [""])[-1], 0) for i in range(n)]
+    todo = {q: [i for i in range(n) if ops[i]["q"] == q] for q in {o["q"] for o in ops}}
+    free, end, order = {q: 0.0 for q in todo}, {}, []
+    while len(order) < n:
+        best = None
+        for q in sorted(todo, key=str):
+            can = [(i, max([free[q]] + [end[j] + WAIT for j in waits[i]])) for i in todo[q]
+                   if all(j in end for j in waits[i] | after[i])]
+            if not can: continue
+            soon = min(t for i, t in can)
+            i, t = max([e for e in can if e[1] <= soon + WAIT], key=lambda e: (way[e[0]], -e[0]))
+            fits = [e for e in can if e[1] + ops[e[0]]["ns"] <= t and e[0] != i]
+            if fits: i, t = max(fits, key=lambda e: (way[e[0]], -e[0]))
+            if best is None or t < best[1]: best = (i, t)
+        i, t = best
+        q = ops[i]["q"]
+        todo[q].remove(i)
+        end[i] = t + ops[i]["ns"]
+        free[q] = t + (ops[i]["ns"] if ops[i]["own"] else 50 if q else 0)
+        order.append(i)
+    return order
+
+
+def emit(g, T, ops):
+    queue = {"v": g.vector, "s": g.scalar, "t": g.tensor, "g": g, "y": g.sync}
+    waits, after = needs(ops)
     needed = set()
-    for d in deps: needed.update(d)
+    for d in waits: needed.update(d)
     count, mark, know, clock = {}, {}, {}, {q: {} for q in queue}
-    for i, o in enumerate(ops):
+    for place, i in enumerate(arrange(ops, waits, after)):
+        o = ops[i]
         q = o["q"]
         if q is None:
-            mark[i], know[i] = (o["sem"], o["n"]), {o["sem"]: o["n"]}
+            mark[i], know[i] = (o["sem"], o["n"], place), {o["sem"]: o["n"]}
             continue
         want = {}
-        for j in deps[i]:
-            s, n = mark[j]
-            if want.get(s, (0, 0))[0] < n: want[s] = (n, j)
-        for s, (n, j) in sorted(want.items(), key=lambda e: -e[1][1]):
+        for j in waits[i]:
+            if j in mark and want.get(mark[j][0], (0,))[0] < mark[j][1]: want[mark[j][0]] = (mark[j][1], mark[j][2], j)
+        for s, (n, _, j) in sorted(want.items(), key=lambda e: -e[1][1]):
             if clock[q].get(s, 0) < n:
                 queue[q].wait_ge(T.sem[s], n)
                 for s2, n2 in know[j].items():
@@ -105,9 +142,10 @@ def emit(g, T, ops):
         if ins is not None and (o["sem"] or i in needed):
             ins.then_inc(T.sem[s], n)
             count[s] = count.get(s, 0) + n
-            mark[i] = (s, count[s])
+            mark[i] = (s, count[s], place)
             know[i] = dict(clock[q])
             know[i][s] = count[s]
+    return count
 
 
 def rank_program(g, core, T, topo):
@@ -119,100 +157,164 @@ def rank_program(g, core, T, topo):
     A, ACT = AluOpType, ActivationFunctionType
     ops = []
 
-    def op(q, f, r=(), w=(), sem=None, n=0):
-        ops.append({"q": q, "f": f, "r": list(r), "w": list(w), "sem": sem, "n": n})
+    def op(q, f, r, w, ns, sem=None, n=0, own=True, on=0):
+        ops.append({"q": q, "f": f, "r": list(r), "w": list(w), "ns": ns, "sem": sem, "n": n, "own": own, "on": on})
 
-    def ts(out, in0, s1, s2, op0, op1, r, w):
-        if s2 is None: op("v", lambda: g.vector.tensor_scalar(out, in0, s1, None, op0), r, w)
-        else: op("v", lambda: g.vector.tensor_scalar(out, in0, s1, s2, op0, op1), r, w)
+    short = lambda n: max(64, n / 2) * CYCLE
+    picked = lambda n: 60 + 1.5 * n * CYCLE
+    spread = lambda n: 50 + 3 * n * CYCLE
 
-    def fill(out, c, w):
-        op("v", lambda: g.vector.memset(out, c), (), w)
+    def ts(out, in0, s1, s2, op0, op1, r, w, ns=short(0)):
+        if s2 is None: op("v", lambda: g.vector.tensor_scalar(out, in0, s1, None, op0), r, w, ns)
+        else: op("v", lambda: g.vector.tensor_scalar(out, in0, s1, s2, op0, op1), r, w, ns)
 
-    def count_up(out, pattern, base, cm, w):
-        op("g", lambda: g.iota(out, pattern, base, cm, allow_small_or_imprecise_dtypes=True), (), w)
+    def tt(out, in0, in1, how, r, w):
+        op("v", lambda: g.vector.tensor_tensor(out, in0, in1, how), r, w, short(0))
 
-    def turn(out, in_, r, w):
-        op("v", lambda: g.vector.transpose(out, in_), r, w)
+    def act(out, in_, func, bias, scale, r, w, n, total=None):
+        op("s", lambda: g.scalar.activation(out, in_, func, bias, scale, accum_out=total), r, w, (64 + n) * CYCLE)
 
-    def scan(out, d0, d1, init, op0, op1, r, w):
-        op("v", lambda: g.vector.tensor_tensor_scan(out, d0, d1, init, op0, op1), r, w)
+    def fill(out, c, w, n=0):
+        op("v", lambda: g.vector.memset(out, c), (), w, short(n))
 
-    def move(q, out, in_, r, w):
-        if q == "v": op("v", lambda: g.vector.tensor_copy(out, in_), r, w)
-        else: op("s", lambda: g.scalar.activation(out, in_, ACT.Copy), r, w)
+    def count_up(out, pattern, base, w, n):
+        op("g", lambda: g.iota(out, pattern, base, 0, allow_small_or_imprecise_dtypes=True), (), w, 130 + 2 * n * CYCLE)
 
-    def quant(codes, plane, in_, r, w):
-        op("v", lambda: g.vector.quantize_mx(codes, plane, in_), r, w)
+    def turn(out, in_, r, w, n=0):
+        op("v", lambda: g.vector.transpose(out, in_), r, w, short(n))
 
-    def product(out, lq, lp, rq, rp, r, w):
-        op("t", lambda: g.tensor.matmul_mx(out, lq, lp, rq, rp, True, True), r, w)
+    def scan(out, d0, d1, init, op0, op1, r, w, n):
+        op("v", lambda: g.vector.tensor_tensor_scan(out, d0, d1, init, op0, op1), r, w, short(n))
 
-    def dma(q, out, in_, sem, r, w):
+    def move(q, out, in_, r, w, ns):
+        if q == "v": op("v", lambda: g.vector.tensor_copy(out, in_), r, w, ns)
+        else: op("s", lambda: g.scalar.activation(out, in_, ACT.Copy), r, w, ns)
+
+    def quant(name, c0, c1, in_, r, w):
+        op("v", lambda: g.vector.quantize_mx(T[name + "q"][:, c0:c1], T[name + "p"][:, c0:c1], in_), r, w, 12 + 0.88 * (c1 - c0))
+
+    def product(out, left, l0, right, c0, c1, r, w):
+        op("t", lambda: g.tensor.matmul_mx(out, T[left + "q"][:, l0:l0 + 128], T[left + "p"][:, l0:l0 + 128],
+                                           T[right + "q"][:, c0:c1], T[right + "p"][:, c0:c1], True, True), r, w, (c1 - c0 + 16) * CYCLE)
+
+    def dma(q, out, in_, sem, r, w, ns, on=0):
         e = g.sync if q == "y" else g.scalar
-        op(q, lambda: e.dma_start(out, in_), r, w, sem)
+        op(q, lambda: e.dma_start(out, in_), r, w, ns, sem, own=False, on=on)
 
     ps = [T["ps%d" % b] for b in range(8)]
     col = lambda i: T.cf[:, i:i + 1]
-    OD, XK, XF, XO, KK = range(5)
+    num = lambda i: T.pi[:, i:i + 1]
+    U1, SC, KB, XK, XF, XG, CP, SAME, Z1, Z2, Z3, MU, GA, BE = range(14)
     sends = rank < n_ranks - 1
-    hc, hn = C // 2, NC // 2
+    far = 100000
 
-    dma("y", T.ub[:, 0:512], T.u[:], "lu", [], ["ub0"])
-    dma("s", T.ub[:, 512:576], T.u[:, 0:64], "lu2", [], ["ub1"])
-    dma("y", T.xb[:, 0:4 * hc], T.x[:, 0:4 * hc], "lx", [], ["xb0"])
-    dma("y", T.xb[:, 4 * hc:4 * C], T.x[:, 4 * hc:4 * C], "lx2", [], ["xb1"])
-    dma("y", T.wq[:].bitcast(dt.uint8), T.wc[:], "lw", [], ["wq"])
-    dma("y", T.wp[:], T.ws[:], "lp", [], ["wp"])
-    dma("y", T.vb[:], T.v[:], "lv", [], ["vb"])
+    dma("y", T.ub[:], T.u[:], "lu", [], ["ub"], 900, 6 * far)
+    for h, (c0, c1) in enumerate(PIECES[0]):
+        dma("y", T.xb[:, 4 * c0:4 * c1], T.x[:, 4 * c0:4 * c1], ("lx", "lx2")[h], [], ["xb%d" % h], 1400 + 350 * h, (5 - h) * far)
+    dma("y", T.wq[:].bitcast(dt.uint8), T.wc[:], "lw", [], ["wq"], 2300, 3 * far)
+    dma("y", T.wp[:], T.ws[:], "lp", [], ["wp"], 2400, 2 * far)
+    dma("y", T.vb[:], T.v[:], "lv", [], ["vb"], 2700, far)
 
-    op("g", lambda: g.iota(T.pi[:, 0:1], [[0, 1]], 0, 1), (), ["pi0"])
-    count_up(T.mv[:], [[16 * int(STEP), 2], [-int(STEP), 32]], int(STEP), 0, ["mv"])
-    count_up(T.s16[:], [[0, NC + 2], [1, 16]], 0, 0, ["s16"])
-    count_up(T.jv[:], [[1, L]], 0, 0, ["jv"])
-    count_up(T.z32[:], [[0, 32]], 0, 0, ["z32"])
-    for b in range(4):
-        count_up(T.pw[:, L * b:L * b + K], [[0, K]], 0, 0, ["pw0%d" % b])
+    op("g", lambda: g.iota(num(0), [[0, 1]], 0, 1), (), ["p"], 132)
+    op("g", lambda: g.iota(num(7), [[0, 1]], 0, 16), (), ["p7"], 132)
+    count_up(T.ui[:], [[32, 4], [-4, 2]], 4, ["ui"], 8)
+    count_up(T.mv[:], [[0, 2], [-1, 32]], 0, ["mv"], 64)
+    count_up(T.bt[:, 0:32], [[0, 32]], -1, ["bt"], 32)
+    count_up(T.zi[:], [[8, 2]], 0, ["zi"], 2)
+    for o in range(2):
+        count_up(T.xe[:, X * o + M:X * o + X], [[0, K]], 0, ["xe2%d" % o], 32)
+    count_up(T.tb[:], [[0, 64]], 0, ["tb"], 64)
+    count_up(T.sel[:, 64 + 31::32], [[0, 33]], 0, ["sel0", "sel1"], 33)
+    count_up(T.pw[:, C::W], [[0, 4]], 0, ["nil"], 4)
+    count_up(T.ji[:], [[32, C // 32], [1, 16]], -C // 2, ["ji"], C // 2)
+    count_up(T.z32[:], [[0, 32]], 0, ["z32"], 32)
+    for t in range(R):
+        count_up(T["inv%d" % t][:], [[0, L]], C // 2, ["inv%d" % t], L)
     if sends:
-        count_up(T.et[:, 128:512], [[0, 384]], 0, 0, ["et0"])
+        count_up(T.et[:, 128:512], [[0, 384]], 0, ["et0"], 384)
     if rank > 0:
-        count_up(T.one[:], [[0, 516]], 1, 0, ["one"])
-        op("g", lambda: g.affine_select(T.one[:], T.one[:], [[-1, 516]], A.is_equal, 0.0, 3, 4), ["one"], ["one"])
+        count_up(T.one[:], [[0, 516]], 1, ["one"], 516)
+        op("g", lambda: g.affine_select(T.one[:], T.one[:], [[-1, 516]], A.is_equal, 0.0, 3, 4), ["one"], ["one"], 170 + 1032 * CYCLE)
 
-    fill(T.hn[:], 0.5, ["hn"])
-    fill(T.dn[:], -STEP, ["dn"])
-    fill(T.zz[:], 0.0, ["zz"])
-    ts(T.pi[:, 1:2], T.pi[:, 0:1], 16, None, A.bitwise_and, None, ["pi0"], ["pi1"])
-    ts(T.pi[:, 2:3], T.pi[:, 0:1], 15, None, A.bitwise_and, None, ["pi0"], ["pi2"])
-    ts(T.pi[:, 3:4], T.pi[:, 0:1], 31, None, A.bitwise_and, None, ["pi0"], ["pi3"])
-    fill(T.hn[:, 0::5], 0.0, ["hn"])
-    fill(T.h0[:], 0.5, ["h0"])
-    odd, lane = T.pi[:, 1:2], T.pi[:, 2:3]
-    ts(col(OD), odd, 15.5 * STEP / 16, STEP, A.mult, A.add, ["pi1"], ["od"])
-    ts(col(XK), lane, STEP, None, A.mult, None, ["pi2"], ["xk"])
-    ts(col(XF), lane, 1.0, None, A.mult, None, ["pi2"], ["xf"])
-    ts(col(XO), lane, -512.0, 7680.0, A.mult, A.add, ["pi2"], ["xo"])
-    ts(col(KK), T.pi[:, 3:4], 2.0, float(C), A.mult, A.add, ["pi3"], ["kk"])
-    for h in range(2):
-        fill(T.xe[:, M * h + L:M * h + M], 0.0, ["xe2%d" % h])
-    ts(T.mt[:, 0:64], T.mv[:], col(XK), 0.0, A.add, A.max, ["mv", "xk"], ["mt0"])
-    ts(T.mt[:, 2 * L:2 * M], T.mv[:], col(XK), 0.0, A.add, A.max, ["mv", "xk"], ["mt2"])
-    turn(T.mk[:, 0:2], T.mt[:, 0:64], ["mt0"], ["mk0"])
-    ts(T.dm[:], T.s16[:], col(XF), -16384.0, A.is_equal, A.mult, ["s16", "xf"], ["dm"])
-    for h in range(2):
-        ts(T.xe[:, M * h:M * h + K], T.mk[:, 0:2, h, :], STEP, None, A.is_equal, None, ["mk0"], ["xe0%d" % h])
-    ts(T.dm[:], T.dm[:], 512.0, None, A.add, None, ["dm"], ["dm"])
-    quant(T.uq[:], T.us[:], T.ub[:], ["ub0", "ub1"], ["uq"])
+    ts(num(1), num(7), 16, None, A.bitwise_and, None, ["p7"], ["p1"])
+    for i, s, m in ((2, 0, 15), (3, 0, 31), (4, 0, 1), (5, 4, 1), (6, 1, 7), (8, 2, 3)):
+        if s: ts(num(i), num(0), s, m, A.logical_shift_right, A.bitwise_and, ["p"], ["p%d" % i])
+        else: ts(num(i), num(0), m, None, A.bitwise_and, None, ["p"], ["p%d" % i])
+    tt(col(U1), num(1), num(8), A.subtract, ["p1", "p8"], ["u1"])
+    ts(T.ul[:], T.ui[:], col(U1), None, A.add, None, ["ui", "u1"], ["ul"])
+    quant("t", 0, 128, T.ub[:], ["ub"], ["tq"])
+    move("v", T.uq[:].bitcast(dt.uint32), T.tq[:].bitcast(dt.uint32).indirect(T.ul[:]), ["tq", "ul"], ["uq"], picked(128))
+    move("s", T.up[:], T.tp[:].indirect(T.ul[:]), ["tq", "ul"], ["up"], picked(128))
+    fill(T.on[:, K:X], 1.0, ["on"], M)
+    fill(T.on[:, K - 1:K], UNIT, ["on1"])
+    for o in range(2):
+        act(T.zz[:, M * o:M * o + M], T.on[:, K:X], ACT.Copy, 0.0, -1.0, ["on"], ["zz%d" % o], M)
+    act(T.dn[:], T.on[:, K:K + 256], ACT.Copy, 0.0, -1.0, ["on"], ["dn"], 256)
+    for t in range(R):
+        act(T["h%d" % t][:], T.on[:, K:K + L], ACT.Copy, 0.0, 0.5, ["on"], ["h%d" % t], L)
+    for i, c in ((None, 2.0), (0, 0.0), (1, 1 / 16), (7, -0.5)):
+        fill(T.hn[:] if i is None else T.hn[:, i::8], c, ["hn"])
+    ts(col(XF), num(2), -1.0, None, A.mult, None, ["p2"], ["xf"])
+    ts(col(XG), num(2), -1.0, -1.0, A.mult, A.add, ["p2"], ["xg"])
+    ts(col(SC), num(3), 20.0, -1.0, A.is_lt, A.mult, ["p3"], ["sc"])
+    ts(col(XK), num(3), 0.5, None, A.add, None, ["p3"], ["xk"])
+    ts(col(KB), num(3), 2 * UNIT, -K * UNIT, A.mult, A.add, ["p3"], ["kb"])
+    ts(col(CP), num(2), 15.0, 1 / LIFT, A.is_equal, A.max, ["p2"], ["cp"])
+    ts(T.s16[:, 16:32], T.mv[:, 0:16], col(XF), None, A.not_equal, None, ["mv", "xf"], ["db"])
+    ts(T.s16[:, 0:16], T.mv[:, 0:16], col(XG), LIFT, A.is_equal, A.mult, ["mv", "xg"], ["da"])
+    ts(T.dl[:], T.mv[:, 0:26], 0.0, col(XF), A.mult, A.subtract, ["mv", "xf"], ["dl"])
+    tt(T.s16[:, 32:48], T.s16[:, 0:16], T.s16[:, 16:32], A.max, ["da", "db"], ["dc"])
+    move("s", T.dm[:], T.s16[:, 32:48].indirect(T.dl[:]), ["dc", "dl"], ["dm"], picked(L))
+    for i, (c0, c1) in enumerate(((0, K), (L, L + 2 * K), (M + L, 2 * M))):
+        ts(T.mt[:, c0:c1], T.mv[:, 0:c1 - c0], col(XK), None, A.add, None, ["mv", "xk"], ["mt%d" % i])
+    for o in range(2):
+        ts(T.xe[:, X * o + K:X * o + 2 * K], T.mt[:, 0:K], 0.5, 2 * UNIT, A.is_equal, A.mult, ["mt0"], ["xe0%d" % o])
+    tt(col(SAME), num(4), num(5), A.is_equal, ["p4", "p5"], ["same"])
+    ts(col(Z1), num(5), 528.0, 63.0, A.mult, A.add, ["p5"], ["z1"])
+    ts(col(Z2), num(5), -16.0, 32.0, A.mult, A.add, ["p5"], ["z2"])
+    ts(col(Z3), num(5), 512.0, 63.0, A.mult, A.add, ["p5"], ["z3"])
+    ts(col(MU), col(SAME), 31.0, 1.0, A.mult, A.add, ["same"], ["mu"])
+    ts(col(GA), col(Z1), col(SAME), col(Z2), A.mult, A.add, ["same", "z1", "z2"], ["ga"])
+    ts(col(BE), num(6), col(MU), col(GA), A.mult, A.add, ["p6", "mu", "ga"], ["be"])
+    ts(T.zl[:, 0:2], T.zi[:], col(MU), col(BE), A.mult, A.add, ["zi", "mu", "be"], ["zl"])
+    ts(T.zl[:, 2:3], num(2), 32.0, col(Z3), A.mult, A.add, ["p2", "z3"], ["za"])
+    ts(T.zl[:, 4:5], num(2), col(Z2), 1.0, A.add, A.add, ["p2", "z2"], ["zb"])
+    ts(T.jv[:, 0:C // 2], T.ji[:], col(Z2), 32.0, A.subtract, A.add, ["ji", "z2"], ["ja"], short(C // 2))
+    ts(T.jv[:, C // 2:C], T.ji[:], col(Z2), -16.0, A.add, A.add, ["ji", "z2"], ["jb"], short(C // 2))
+    quant("v", 0, 128, T.vb[:], ["vb"], ["vq"])
+    if rank > 0:
+        fill(T.ct[:], 0.0, ["ct"], 512)
+        for b in range(4):
+            quant("i", 128 * b, 128 * b + 128, T.one[:, 3 - b:515 - b], ["one"], ["i%d" % b])
+        quant("l", 96, 224, T.ct[:], ["ct"], ["lz"])
+        if rank > 2:
+            for s in range(2):
+                fill(T.cm[:, K * s:K * s + K], 0.5 ** (2 - s), ["cm%d" % s])
 
     def state(t, h, tile, r):
-        c = slice(hc * h, hc * h + hc)
-        quant(T["aq%d" % t][:, c], T["ap%d" % t][:, c], tile[:, 4 * hc * h:4 * hc * h + 4 * hc], r, ["a%d%d" % (t, h)])
+        c0, c1 = PIECES[t][h]
+        an, a = "a%d" % t, "a%d%d" % (t, h)
+        quant(an, c0, c1, tile[:, 4 * c0:4 * c1], r, [a])
+        if t < R:
+            product(ps[h][:, 0:c1 - c0], "u", 0, an, c0, c1, ["uq", "up", a], ["ps%d" % h])
+            act(T.b2[:, c0:c1], ps[h][:, 0:c1 - c0], ACT.Sign, -TINY, col(SC), ["sc"], ["ps%d" % h, "b2%d" % h], c1 - c0)
+        else:
+            product(ps[h][:, 0:c1 - c0], "v", 0, an, c0, c1, ["vq", a], ["ps%d" % h])
+            dma("y", T.oc[:, 4 * c0:4 * c1], T[an + "q"][:, c0:c1].bitcast(dt.uint8), "oc", [a], [], 1000)
+            if h:
+                for k in range(4):
+                    dma("ys"[k % 2], T.osc[4 * k:4 * k + 4, :], T[an + "p"][32 * k:32 * k + 4, :], ("oc", "oy")[k % 2], [an + "0", a], [], 800)
+            move("sv"[h], T.yb[:, c0:c1], ps[h][:, 0:c1 - c0], [], ["ps%d" % h, "y%d" % h], (c1 - c0) * CYCLE)
+            dma("s", T.y[:, c0:c1], T.yb[:, c0:c1], "oy", ["y%d" % h], [], 1000)
 
     calls = plan_calls(topo, cores, rank)
     sent = [0]
 
     def landing(t, d, s):
         return (96 - K * d if t == 0 else 224) + K * s
+
+    def early(t, d, s):
+        return t > 0 and s == 0 and d > 1
 
     def send(t):
         order = calls
@@ -226,188 +328,131 @@ def rank_program(g, core, T, topo):
                         a = landing(t, d, rank)
                         rid, pid = topo.addr(cores[d])[0:2]
                         if part == 0:
-                            src, dst = T["eq%d" % t][:, 0:K].bitcast(dt.uint8), T.lq[:, a:a + K].bitcast(dt.uint8)
+                            src, dst = T["e%dq" % t][:, 0:K].bitcast(dt.uint8), T.lq[:, a:a + K].bitcast(dt.uint8)
                         else:
-                            src, dst = T["ep%d" % t][:, 0:K], T.lp[:, a:a + K]
+                            src, dst = T["e%dp" % t][:, 0:K], T.lp[:, a:a + K]
                         tr.append(RemoteDMATransfer(dst_ids=[DstId(rid=rid, pnc=pid)], dma_engine_mask=sum(1 << e for e in es),
-                                                    remote_sem=T.sem["arr%d" % t], src=src, dst=dst))
+                                                    remote_sem=T.sem["arr%d" % (t + early(t, d, rank))], src=src, dst=dst))
                         sent[0] += len(es)
                     g.remote_dma_fused(tr, local_sem=T.sem.sent)
-                op("g", issue, ["e%d" % t], [])
+                op("g", issue, ["e%d" % t], ["calls"], 200, on=(R - t) * 20000 * (rank == 0))
 
-    arriving = 2 * sum(len(es) for s in range(rank) for call in plan_calls(topo, cores, s) for d, es in call if d == rank)
-    slots, ends = T.pl[:, 0:2], T.pl[:, NC + 2:NC + 4]
+    def arriving(t, soon):
+        return 2 * sum(len(es) for s in range(rank) for call in plan_calls(topo, cores, s) for d, es in call
+                       if d == rank and early(t, d, s) == soon)
+
+    slots, ends = T.pl[:, 0:2], T.pl[:, 26:28]
     plane = lambda buf, b: buf[:, L * b:L * b + L]
 
     def one_round(t):
-        aq, ap, a = T["aq%d" % t], T["ap%d" % t], ["a%d0" % t, "a%d1" % t]
-        half, hk = T["h%d" % t], "h%d" % t
-
-        def signs(h):
-            c, k = slice(hc * h, hc * h + hc), slice(hn * h, hn * h + hn)
-            for o in (1, 0):
-                product(ps[2 * h + o][:, 0:hc], T.uq[:, 16 * o:16 * o + 128], T.us[:, 16 * o:16 * o + 128], aq[:, c], ap[:, c],
-                        ["uq", a[h]], ["ps%d" % (2 * h + o)])
-            ts(T.b2[:, k, 0, :], ps[2 * h][:, 0:hc], 0.0, 2.0, A.is_lt, A.mult, [], ["ps%d" % (2 * h), "b20%d" % h])
-            op("s", lambda: g.scalar.activation(T.b2[:, k, 1, :], ps[2 * h + 1][:, 0:hc], ACT.Sign, -TINY, -1.0),
-               [], ["ps%d" % (2 * h + 1), "b21%d" % h])
-
-        def bits(h):
-            k = slice(hn * h, hn * h + hn)
-            turn(T.bt[:, k], T.b2[:, k], ["b20%d" % h, "b21%d" % h], ["bt%d" % h])
-
-        def five(h):
-            move("v", T.b5[:, 5 * hn * h:5 * hn * (h + 1)], T.bt[:, hn * h:hn * h + hn, 0:5], ["bt%d" % h], ["b5%d" % h])
-
-        def key(h):
-            c = slice(5 * hn * h, 5 * hn * (h + 1))
-            scan(T.ky[:, c], T.hn[:, c], T.b5[:, c], 0.0, A.mult, A.add, ["hn", "b5%d" % h], ["ky%d" % h])
-
-        def head(h):
-            ts(T.zz[:, C * h:C * h + C:32], T.ky[:, 5 * hn * h + 4:5 * hn * (h + 1):5], 8 * STEP, col(OD), A.mult, A.add,
-               ["ky%d" % h, "od", "zz"], ["zz%d" % h])
-
-        def down(h):
-            scan(T.mt[:, 64 + C * h:64 + C * h + C], T.dn[:], T.zz[:, C * h:C * h + C], 0.0, A.add, A.max,
-                 ["dn", "zz", "zz%d" % h], ["mt1%d" % h])
-
-        def by_key(h):
-            turn(T.mk[:, 2 + hn * h:2 + hn * h + hn], T.mt[:, 64 + C * h:64 + C * h + C], ["mt1%d" % h], ["mk1%d" % h])
-
-        def own(o, h):
-            ts(T.xe[:, M * o + K + hc * h:M * o + K + hc * h + hc], T.mk[:, 2 + hn * h:2 + hn * h + hn, o, :], STEP, None, A.is_equal, None,
-               ["mk1%d" % h], ["xe1%d%d" % (o, h)])
-
-        if t == 0: state(0, 0, T.xb, ["xb0"])
-        signs(0)
-        if t == 0: state(0, 1, T.xb, ["xb1"])
-        bits(0); signs(1)
+        an, a = "a%d" % t, ["a%d0" % t, "a%d1" % t]
+        half, hk, inv, ik = T["h%d" % t], "h%d" % t, T["inv%d" % t], "inv%d" % t
         for b in range(4):
-            product(ps[4 + b][:, 0:C], T.wq[:, 128 * b:128 * b + 128], T.wp[:, 128 * b:128 * b + 128], aq[:], ap[:],
-                    ["wq", "wp"] + a, ["ps%d" % (4 + b)])
-        five(0); bits(1); key(0); five(1); head(0); key(1); down(0); head(1); by_key(0); down(1)
-        own(0, 0); by_key(1); own(1, 0); own(0, 1); own(1, 1)
+            product(ps[4 + b][:, 0:C], "w", 128 * b, an, 0, C, ["wq", "wp"] + a, ["ps%d" % (4 + b)])
+            act(T.pw[:, W * b:W * b + C], ps[4 + b][:, 0:C], ACT.Copy, 0.0, 0.03125, [], ["ps%d" % (4 + b), "pw%d" % b], C)
+        for h, (c0, c1) in enumerate(PIECES[t]):
+            n = c1 - c0
+            turn(T.bt[:, K + c0:K + c1], T.b2[:, c0:c1], ["b2%d" % h], ["bt%d" % h], n)
+            for o in range(2):
+                z, oh = M * o + c0 + K * h, "%d%d" % (o, h)
+                scan(T.zz[:, z + 4:z + 4 + n:4], T.hn[:, 0:n // 4], T.bt[:, K - 8 + c0 + o:K - 8 + c1:4], 0.0, A.mult, A.add,
+                     ["hn", "zz%d" % o, "bt", "bt0", "bt%d" % h], ["zz" + oh], 0)
+                scan(T.mt[:, M * o + K + c0:M * o + K + c1], T.dn[:, 0:n], T.zz[:, z + K:z + K + n], 0.0, A.add, A.max,
+                     ["dn", "zz%d" % o, "zz" + oh], ["mt" + oh], n)
+                mk = T.mk[:, C * o + c0:C * o + c1]
+                turn(mk, T.mt[:, M * o + K + c0:M * o + K + c1], ["mt" + oh], ["mk" + oh], n)
+                ts(T.xe[:, X * o + 2 * K + c0:X * o + 2 * K + c1], mk, 0.5, 2 * UNIT, A.is_equal, A.mult, ["mk" + oh], ["xe1" + oh], short(n))
+                act(T.sg[:, C * o + c0:C * o + c1], mk, ACT.Sign, 0.0, -1.0, ["mk" + oh], ["sg" + oh, "acc" + oh], n + 24,
+                    T.acc[:, 2 * o + h:2 * o + h + 1])
         for o in range(2):
-            op("s", lambda o=o: g.scalar.activation(T.sg[:, C * o:C * o + C], T.mk[:, 2:NC + 2, o, :], ACT.Sign, 512.0, -1.0,
-                                                    accum_out=T.acc[:, o:o + 1]), ["mk10", "mk11"], ["sg%d" % o, "acc%d" % o])
-        for b in range(4):
-            op("s", lambda b=b: g.scalar.activation(T.pw[:, L * b + K:L * b + L], ps[4 + b][:, 0:C], ACT.Copy, 0.0, 0.03125),
-               [], ["ps%d" % (4 + b), "pw1%d" % b])
-        for o in range(2):
-            xe = T.xe[:, M * o:M * o + M]
-            scan(T.cu[:, M * o:M * o + M], xe, xe, -float(L), A.add, A.add,
-                 ["xe0%d" % o, "xe1%d0" % o, "xe1%d1" % o, "xe2%d" % o], ["cu%d" % o])
-        hm, hs = M // 2, hn + 2
-        for o in range(2):
-            for h in range(2):
-                ts(T.st[:, hs * h:hs * h + hs, o, :], T.cu[:, M * o + hm * h:M * o + hm * h + hm], T.acc[:, o:o + 1], col(KK), A.add, A.add,
-                   ["kk", "cu%d" % o, "acc%d" % o], ["st%d%d" % (o, h)])
-        for h in range(2):
-            turn(T.stt[:, M * h:M * h + M], T.st[:, hs * h:hs * h + hs], ["st0%d" % h, "st1%d" % h], ["stt%d" % h])
-        for h in range(2):
-            scan(T.sel[:, M * h:M * h + M], T.mt[:, M * h:M * h + M], T.stt[:, M * h:M * h + M], 0.0, A.add, A.min,
-                 ["mt0", "mt1%d" % h, "mt2", "stt%d" % h], ["sel%d" % h])
-        ts(T.pl[:], T.sel[:, 31::32], 0.5, L / 2 - 1.0, A.mult, A.add, ["sel0", "sel1"], ["pl"])
-        move("v", T.inv[:].indirect(T.pl[:, 0:NC + 2]), T.jv[:], ["pl", "jv"], ["inv"])
-        scan(T.dg[:], T.dm[:], T.inv[:], 0.0, A.add, A.max, ["dm", "inv"], ["dg"])
-        ts(T.il[:], T.dg[:, 15::16], col(XO), None, A.subtract, None, ["dg", "xo"], ["il"])
-        move("v", half[:].indirect(slots), T.z32[:], ["pl", "z32"], [hk])
+            ts(T.xe[:, X * o + K - 1:X * o + K], T.acc[:, 2 * o:2 * o + 1], UNIT, col(KB), A.mult, A.add, ["kb", "acc%d0" % o], ["xl%d" % o])
+            scan(T.cu[:, X * o + K - 1:X * o + X], T.on[:, K - 1:X], T.xe[:, X * o + K - 1:X * o + X], T.acc[:, 2 * o + 1:2 * o + 2], A.mult, A.add,
+                 ["on", "on1", "xl%d" % o, "xe0%d" % o, "xe1%d0" % o, "xe1%d1" % o, "xe2%d" % o, "acc%d1" % o], ["cu%d" % o], M)
+            turn(T.st[:, M * o:M * o + M], T.cu[:, X * o + K:X * o + X], ["cu%d" % o], ["st%d" % o], M)
+            scan(T.sel[:, 64 + 512 * o:64 + 512 * o + M], T.mt[:, M * o:M * o + M], T.st[:, M * o:M * o + M], 0.0, A.max, A.min,
+                 ["mt0", "mt1", "mt2", "mt%d0" % o, "mt%d1" % o, "st%d" % o], ["sel%d" % o], M)
+        turn(T.tb[:, 16:48], T.sel[:, 64 + 31:64 + 1024:32], ["sel0", "sel1"], ["tb"])
+        turn(T.sel[:, 0:64], T.tb[:], ["tb"], ["sel2"])
 
-        def sort(q, b, c0=0, c1=NC + 2, tag=""):
-            w = ["pz%d%s" % (b, x) for x in (tag or "ab")]
-            move(q, T.pz[:, L * b + 16 * c0:L * b + 16 * c1], plane(T.pw, b).indirect(T.il[:, c0:c1]),
-                 ["il", "pw0%d" % b, "pw1%d" % b], w)
+        def places(out, c0, c1, lst, r, w, n):
+            ts(out, T.sel[:, c0:c1].indirect(lst), 0.5 / UNIT, L / 2 - 1.0, A.mult, A.add, r, w, picked(n))
+
+        places(T.pa[:, 0:16], 64, 1120, T.zl[:, 2:3], ["za", "sel0", "sel1"], ["pa"], 16)
+        places(T.pa[:, 16:32], 0, 64, T.zl[:, 4:5], ["zb", "sel2"], ["pb"], 16)
+        places(T.pl[:], 0, 1120, T.zl[:, 0:2], ["zl", "sel0", "sel1", "sel2"], ["pl"], 32)
+        for i, r in enumerate("ab"):
+            move("v", inv[:].indirect(T.pa[:, 16 * i:16 * i + 12]), T.jv[:, 192 * i:192 * i + 192], ["p" + r, "j" + r], [ik], spread(192))
+        move("v", half[:].indirect(slots), T.z32[:], ["pl", "z32"], [hk], spread(K))
+        scan(T.dg[:], T.dm[:], inv[:], 0.0, A.mult, A.add, ["dm", ik], ["dg"], L)
+        ts(T.il[:], T.dg[:, 15::16], col(CP), C / 2, A.mult, A.add, ["dg", "cp"], ["il"])
+
+        made = {b: [] for b in range(4)}
+        for b, q, c0, c1 in SORT:
+            made[b].append("pz%d_%d" % (b, len(made[b])))
+            move(q, T.pz[:, L * b + 16 * c0:L * b + 16 * c1], T.pw[:, W * b:W * b + W].indirect(T.il[:, c0:c1]),
+                 ["il", "nil", "pw%d" % b], [made[b][-1]], picked(16 * (c1 - c0)))
 
         def run(b):
-            scan(plane(T.hs, b), half[:], plane(T.pz, b), 0.0, A.mult, A.max, [hk, "pz%da" % b, "pz%db" % b], ["hs%d" % b])
-
-        def last(q, b):
-            move(q, T.et[:, b:128:4], plane(T.hs, b).indirect(ends), ["pl", "hs%d" % b], ["et1%d" % b])
-
-        def unsort(q, b, h0=0, h1=2):
-            move(q, T.ht[:, 4 * hc * h0 + b:4 * hc * h1:4], plane(T.hs, b).indirect(T.pl[:, 2 + hn * h0:2 + hn * h1]),
-                 ["pl", "hs%d" % b], ["ht%d%d" % (b, h) for h in range(h0, h1)])
-
-        def new_state():
-            unsort("s", 0); unsort("s", 1, 0, 1); unsort("v", 2, 0, 1); unsort("s", 3, 0, 1)
-            state(t + 1, 0, T.ht, ["ht%d0" % b for b in range(4)])
-            unsort("s", 1, 1, 2); unsort("v", 2, 1, 2); unsort("s", 3, 1, 2)
-            state(t + 1, 1, T.ht, ["ht%d1" % b for b in range(4)])
+            scan(plane(T.hs, b), half[:], plane(T.pz, b), 0.0, A.mult, A.max, [hk] + made[b], ["hs%d" % b], L)
 
         if sends:
-            sort("s", 0); sort("v", 2); sort("s", 1)
-            sort("v", 3, 0, 14, "a"); sort("s", 3, 14, NC + 2, "b")
-            run(2); run(0); run(1); run(3)
-            last("s", 2); last("s", 0); last("s", 1); last("v", 3)
-            quant(T["eq%d" % t][:], T["ep%d" % t][:], T.et[:], ["et0"] + ["et1%d" % b for b in range(4)], ["e%d" % t])
+            for b in (2, 0, 1, 3):
+                run(b)
+                move("sssv"[b], T.et[:, b:128:4], plane(T.hs, b).indirect(ends), ["pl", "hs%d" % b], ["et1%d" % b], picked(K))
+            quant("e%d" % t, 0, 128, T.et[:], ["et0"] + ["et1%d" % b for b in range(4)], ["e%d" % t])
             send(t)
-        else:
-            sort("s", 0); sort("v", 2); sort("s", 1); sort("v", 3)
 
-        if rank == 0:
-            new_state()
-        if t == 0:
-            if rank > 0:
-                fill(T.ct[:], 0.0, ["ct"])
-                for b in range(4):
-                    quant(T.iq[:, 128 * b:128 * b + 128], T.ip[:, 128 * b:128 * b + 128], T.one[:, 3 - b:515 - b], ["one"], ["i%d" % b])
-                quant(T.lq[:, 96:224], T.lp[:, 96:224], T.ct[:], ["ct"], ["lz"])
-                if rank > 1:
-                    for s in range(rank):
-                        fill(T.cm[:, K * s:K * s + K], 0.5 ** (rank - 1 - s), ["cm%d" % s])
-            fill(T.h1[:], 0.5, ["h1"])
-            quant(T.vq[:], T.vs[:], T.vb[:], ["vb"], ["vq"])
         if rank > 0:
-            op(None, None, [], ["land%d" % t], "arr%d" % t, arriving)
-            v0 = 96 - K * rank if t == 0 else 96 + K * rank
-            e0 = landing(t, rank, 0) - v0
-            n = K * rank
-            for b in range(4):
-                product(ps[b][:, 0:128], T.iq[:, 128 * b:128 * b + 128], T.ip[:, 128 * b:128 * b + 128],
-                        T.lq[:, v0:v0 + 128], T.lp[:, v0:v0 + 128], ["i%d" % b, "lz", "land%d" % t], ["ps%d" % b])
-            if rank == 1:
-                for b in range(4):
-                    move("sv"[b % 2], T.ct[:, b:128:4], ps[b][:, e0:e0 + K], ["ct"], ["ps%d" % b, "ct%d" % b])
-                made = ["ct%d" % b for b in range(4)]
-            else:
-                for b in range(4):
-                    op("v", lambda b=b: g.vector.tensor_tensor(T.dd[:, b:4 * n:4], ps[b][:, e0:e0 + n], T.cm[:, 0:n], A.mult),
-                       ["cm%d" % s for s in range(rank)], ["ps%d" % b, "dd%d" % b])
-                dd = ["dd%d" % b for b in range(4)]
-                prev, pk = T.dd[:, 0:128], []
-                for s in range(1, rank):
-                    out, ok = (T.ct[:, 0:128], "ct0") if s == rank - 1 else (T.d2[:], "d2")
-                    op("v", lambda out=out, prev=prev, s=s: g.vector.tensor_tensor(out, prev, T.dd[:, 128 * s:128 * s + 128], A.max),
-                       dd + pk + ["ct"], [ok])
-                    prev, pk = out, [ok]
-                made = ["ct0"]
-            quant(T.cq[:], T.cp[:], T.ct[:], ["ct"] + made, ["cq"])
-            for b in range(4):
-                product(ps[4 + b][:, 0:128], T.iq[:, 128 * b:128 * b + 128], T.ip[:, 128 * b:128 * b + 128],
-                        T.cq[:], T.cp[:], ["i%d" % b, "cq"], ["ps%d" % (4 + b)])
-            for b in range(4):
-                move("s", T.cc[:, K * b:K * b + K], ps[4 + b][:, 0:K], [], ["ps%d" % (4 + b), "cc%d" % b])
-            for b in range(5):
-                if b < 4:
-                    move("v", plane(T.pz, b).indirect(slots), T.cc[:, K * b:K * b + K], ["pl", "cc%d" % b], ["pz%da" % b, "pz%db" % b])
-                if b > 0: run(b - 1)
-            new_state()
+            def unpack(b, v0, r):
+                product(ps[b][:, 0:128], "i", 128 * b, "l", v0, v0 + 128, ["i%d" % b, "lz"] + r, ["ps%d" % b])
 
+            soon = early(t, rank, 0)
+            if soon:
+                op(None, None, a, ["soon"], 3000, "arr%d" % (t + 1), arriving(t, True), False)
+                for b in range(4):
+                    unpack(b, landing(t, rank, 0) - 96, ["soon"])
+                    act(T.d2[:, K * b:K * b + K], ps[b][:, 96:128], ACT.Copy, 0.0, 0.5 ** (rank - 1), [], ["ps%d" % b, "d2%d" % b], K)
+            op(None, None, ["e%d" % t] if sends else [made[b][-1] for b in range(4)], ["land%d" % t], 2000 if sends else 3500,
+               "arr%d" % t, arriving(t, False), False)
+            v0 = 96 - K * rank if t == 0 else 96 + K * rank
+            end = lambda b, s, n=1: ps[b][:, landing(t, rank, s) - v0:landing(t, rank, s) - v0 + K * n]
+            for b in range(4):
+                unpack(b, v0, ["land%d" % t, "soon"])
+                out, pb, d0, d1, d2 = T.ct[:, b:128:4], "ps%d" % b, T.dd[:, 64 * b:64 * b + K], T.dd[:, 64 * b + K:64 * b + 64], T.d2[:, K * b:K * b + K]
+                if rank == 1:
+                    move("v", out, end(b, 0), ["ct"], [pb, "ct%d" % b], short(0))
+                elif rank == 2 and soon:
+                    tt(out, d2, end(b, 1), A.max, ["ct", "d2%d" % b], [pb, "ct%d" % b])
+                elif rank == 2:
+                    ts(d0, end(b, 0), 0.5, None, A.mult, None, [], [pb, "dd%d" % b])
+                    tt(out, d0, end(b, 1), A.max, ["ct", "dd%d" % b], [pb, "ct%d" % b])
+                elif soon:
+                    ts(d0, end(b, 1), 0.5, None, A.mult, None, [], [pb, "dd%d" % b])
+                    tt(d1, d2, end(b, 2), A.max, ["d2%d" % b], [pb, "de%d" % b])
+                    tt(out, d0, d1, A.max, ["ct", "dd%d" % b, "de%d" % b], ["ct%d" % b])
+                else:
+                    tt(T.dd[:, 64 * b:64 * b + 64], end(b, 0, 2), T.cm[:], A.mult, ["cm0", "cm1"], [pb, "dd%d" % b, "de%d" % b])
+                    tt(d2, d0, end(b, 2), A.max, ["dd%d" % b], [pb, "d2%d" % b])
+                    tt(out, d1, d2, A.max, ["ct", "de%d" % b, "d2%d" % b], ["ct%d" % b])
+            quant("c", 0, 128, T.ct[:], ["ct"] + ["ct%d" % b for b in range(4)], ["cq"])
+            for b in range(4):
+                product(ps[4 + b][:, 0:128], "i", 128 * b, "c", 0, 128, ["i%d" % b, "cq"], ["ps%d" % (4 + b)])
+                move("s", T.cc[:, K * b:K * b + K], ps[4 + b][:, 0:K], [], ["ps%d" % (4 + b), "cc%d" % b], 96 * CYCLE)
+                move("v", plane(T.pz, b).indirect(slots), T.cc[:, K * b:K * b + K], ["pl", "cc%d" % b], made[b], spread(K))
+                run(b)
+        for h, (c0, c1) in enumerate(PIECES[t + 1]):
+            for b in range(4):
+                move(UNSORT[t][h][b], T.ht[:, 4 * c0 + b:4 * c1:4], plane(T.hs, b).indirect(T.pl[:, 2 + c0 // 16:2 + c1 // 16]),
+                     ["pl", "hs%d" % b], ["ht%d%d" % (b, h)], picked(c1 - c0))
+            state(t + 1, h, T.ht, ["ht%d%d" % (b, h) for b in range(4)])
+
+    for h in range(2):
+        state(0, h, T.xb, ["xb%d" % h])
     for t in range(R):
         one_round(t)
 
-    aq, ap, a = T["aq%d" % R], T["ap%d" % R], ["a%d0" % R, "a%d1" % R]
-    for h in range(2):
-        c = slice(hc * h, hc * h + hc)
-        product(ps[h][:, 0:hc], T.vq[:], T.vs[:], aq[:, c], ap[:, c], ["vq", a[h]], ["ps%d" % h])
-        dma("y", T.oc[:, 4 * hc * h:4 * hc * h + 4 * hc], aq[:, c].bitcast(dt.uint8), "oc", [a[h]], [])
-        move("s", T.yb[:, c], ps[h][:, 0:hc], [], ["ps%d" % h, "y%d" % h])
-        dma("s", T.y[:, c], T.yb[:, c], "oy", ["y%d" % h], [])
-    for k in range(4):
-        dma("y", T.osc[4 * k:4 * k + 4, :], ap[32 * k:32 * k + 4, :], "oc", a, [])
-
-    emit(g, T, ops)
-    g.sync.wait_ge(T.sem.oc, 16 * 6)
-    g.scalar.wait_ge(T.sem.oy, 16 * 2)
+    count = emit(g, T, ops)
+    g.sync.wait_ge(T.sem.oc, count["oc"])
+    g.scalar.wait_ge(T.sem.oy, count["oy"])
     if sent[0]:
         g.wait_ge(T.sem.sent, sent[0])

from concourse.bass import DstId, RemoteDMATransfer
from concourse.mybir import dt, AluOpType, ActivationFunctionType

C, K, R = 384, 32, 2
L = C + K
M = L + K
X = M + K
W = C + 16
UNIT = 2.0 ** -10
LIFT = 2.0 ** 14
TINY = 2.0 ** -126
CODES, BF, F32, U16 = "float8_e4m3fn_x4", "bfloat16", "float32", "uint16"

PIECES = [((0, c), (c, C)) for c in (192, 224, 192)]
SORT = ((0, "s", 0, 26), (2, "v", 0, 26), (1, "s", 0, 26), (3, "v", 0, 18), (3, "s", 18, 26))
UNSORT = [("sssv", "ssvv"), ("ssvv", "sssv")]
WAIT = 250
CYCLE = 0.83
AHEAD = {"tb": 300, "sel2": 600}

SCRATCH = {
    "xb": ("sbuf", [128, 4 * C], BF), "ub": ("sbuf", [128, 512], BF), "vb": ("sbuf", [128, 512], BF),
    "pi": ("sbuf", [128, 10], "int32"), "cf": ("sbuf", [128, 16], F32), "acc": ("sbuf", [128, 4], F32),
    "ui": ("sbuf", [128, 8], F32), "ul": ("sbuf", [128, 8], U16), "zi": ("sbuf", [128, 2], F32), "zl": ("sbuf", [128, 6], U16),
    "mv": ("sbuf", [128, 64], BF), "s16": ("sbuf", [128, 48], BF), "dm": ("sbuf", [128, L], BF), "dl": ("sbuf", [128, 26], U16),
    "ji": ("sbuf", [128, C // 2], BF), "jv": ("sbuf", [128, C], BF),
    "one": ("sbuf", [128, 516], BF), "z32": ("sbuf", [128, 32], BF), "on": ("sbuf", [128, X], BF),
    "b2": ("sbuf", [128, C], BF), "bt": ("sbuf", [128, L], BF), "hn": ("sbuf", [128, 64], BF),
    "zz": ("sbuf", [128, 2 * M], BF), "dn": ("sbuf", [128, 256], BF),
    "mt": ("sbuf", [128, 2 * M], BF), "mk": ("sbuf", [128, 2 * C], BF), "sg": ("sbuf", [128, 2 * C], BF),
    "xe": ("sbuf", [128, 2 * X], BF), "cu": ("sbuf", [128, 2 * X], BF), "st": ("sbuf", [128, 2 * M], BF),
    "sel": ("sbuf", [128, 64 + 1056], BF), "tb": ("sbuf", [128, 64], BF),
    "pl": ("sbuf", [128, 32], U16), "pa": ("sbuf", [128, 32], U16), "il": ("sbuf", [128, 26], U16), "dg": ("sbuf", [128, L], BF),
    "pw": ("sbuf", [128, 4 * W], BF), "pz": ("sbuf", [128, 4 * L], BF), "hs": ("sbuf", [128, 4 * L], BF),
    "et": ("sbuf", [128, 512], BF), "ct": ("sbuf", [128, 512], BF), "ht": ("sbuf", [128, 4 * C], BF),
    "cm": ("sbuf", [128, 64], BF), "dd": ("sbuf", [128, 256], BF), "d2": ("sbuf", [128, 128], BF), "cc": ("sbuf", [128, 128], BF),
    "yb": ("sbuf", [128, C], F32),
}
for _n, _w in (("t", 128), ("u", 128), ("v", 128), ("w", 512), ("i", 512), ("l", 320), ("c", 128),
               ("a0", C), ("a1", C), ("a2", C), ("e0", 128), ("e1", 128)):
    SCRATCH[_n + "q"] = ("sbuf", [128, _w], CODES)
    SCRATCH[_n + "p"] = ("sbuf", [128, _w], "uint8")
for _t in range(R):
    SCRATCH["h%d" % _t] = ("sbuf", [128, L], BF)
    SCRATCH["inv%d" % _t] = ("sbuf", [128, L], BF)
for _t in range(8):
    SCRATCH["ps%d" % _t] = ("psum", [128, 512], F32)

SEMAPHORES = ["cv", "cs", "ct", "cg", "lu", "lx", "lx2", "lw", "lp", "lv", "oy", "oc", "sent", "arr0", "arr1", "arr2"]


def plan_calls(topo, cores, r):
    src = cores[r]
    later = list(range(r + 1, len(cores)))
    if not later:
        return []
    width = min(len(topo.engines(src, cores[d])) for d in range(len(cores)) if d != r)
    calls = []
    for d in later:
        can = topo.engines(src, cores[d])
        for call in calls:
            used = [e for _, es in call for e in es]
            free = [e for e in can if e not in used]
            if len(free) >= width:
                call.append((d, free[-width:]))
                break
        else:
            calls.append([(d, can[-width:])])
    return calls


def needs(ops):
    writers, readers, waits, after = {}, {}, [], []
    for i, o in enumerate(ops):
        d, a = set(), set()
        for k in o["r"]:
            d.update(writers.get(k, []))
        for k in o["w"]:
            for j in writers.get(k, []) + readers.get(k, []):
                (a if ops[j]["q"] == o["q"] and (k == "calls" or k[:2] == "ps" and o["q"] != "t") else d).add(j)
        for k in o["r"]:
            readers.setdefault(k, []).append(i)
        for k in o["w"]:
            writers[k] = [j for j in writers.get(k, []) if j in a] + [i]
            readers[k] = []
        waits.append(d - {i})
        after.append(a - d - {i})
    return waits, after


def arrange(ops, waits, after):
    n = len(ops)
    way = [o["ns"] + o["on"] for o in ops]
    for i in range(n - 1, -1, -1):
        for j in waits[i]: way[j] = max(way[j], ops[j]["ns"] + WAIT + way[i])
        for j in after[i]: way[j] = max(way[j], ops[j]["ns"] + way[i])
    way = [way[i] + AHEAD.get((ops[i]["w"] or [""])[-1], 0) for i in range(n)]
    todo = {q: [i for i in range(n) if ops[i]["q"] == q] for q in {o["q"] for o in ops}}
    free, end, order = {q: 0.0 for q in todo}, {}, []
    while len(order) < n:
        best = None
        for q in sorted(todo, key=str):
            can = [(i, max([free[q]] + [end[j] + WAIT for j in waits[i]])) for i in todo[q]
                   if all(j in end for j in waits[i] | after[i])]
            if not can: continue
            soon = min(t for i, t in can)
            i, t = max([e for e in can if e[1] <= soon + WAIT], key=lambda e: (way[e[0]], -e[0]))
            fits = [e for e in can if e[1] + ops[e[0]]["ns"] <= t and e[0] != i]
            if fits: i, t = max(fits, key=lambda e: (way[e[0]], -e[0]))
            if best is None or t < best[1]: best = (i, t)
        i, t = best
        q = ops[i]["q"]
        todo[q].remove(i)
        end[i] = t + ops[i]["ns"]
        free[q] = t + (ops[i]["ns"] if ops[i]["own"] else 50 if q else 0)
        order.append(i)
    return order


def emit(g, T, ops):
    queue = {"v": g.vector, "s": g.scalar, "t": g.tensor, "g": g, "y": g.sync}
    waits, after = needs(ops)
    needed = set()
    for d in waits: needed.update(d)
    count, mark, know, clock = {}, {}, {}, {q: {} for q in queue}
    for place, i in enumerate(arrange(ops, waits, after)):
        o = ops[i]
        q = o["q"]
        if q is None:
            mark[i], know[i] = (o["sem"], o["n"], place), {o["sem"]: o["n"]}
            continue
        want = {}
        for j in waits[i]:
            if j in mark and want.get(mark[j][0], (0,))[0] < mark[j][1]: want[mark[j][0]] = (mark[j][1], mark[j][2], j)
        for s, (n, _, j) in sorted(want.items(), key=lambda e: -e[1][1]):
            if clock[q].get(s, 0) < n:
                queue[q].wait_ge(T.sem[s], n)
                for s2, n2 in know[j].items():
                    if clock[q].get(s2, 0) < n2: clock[q][s2] = n2
        ins = o["f"]()
        s, n = (o["sem"], 16) if o["sem"] else ("c" + q, 1)
        if ins is not None and (o["sem"] or i in needed):
            ins.then_inc(T.sem[s], n)
            count[s] = count.get(s, 0) + n
            mark[i] = (s, count[s], place)
            know[i] = dict(clock[q])
            know[i][s] = count[s]
    return count


def rank_program(g, core, T, topo):
    rank = T.rank_of(core)
    if rank is None:
        return
    cores = list(T.cores)
    n_ranks = len(cores)
    A, ACT = AluOpType, ActivationFunctionType
    ops = []

    def op(q, f, r, w, ns, sem=None, n=0, own=True, on=0):
        ops.append({"q": q, "f": f, "r": list(r), "w": list(w), "ns": ns, "sem": sem, "n": n, "own": own, "on": on})

    short = lambda n: max(64, n / 2) * CYCLE
    picked = lambda n: 60 + 1.5 * n * CYCLE
    spread = lambda n: 50 + 3 * n * CYCLE

    def ts(out, in0, s1, s2, op0, op1, r, w, ns=short(0)):
        if s2 is None: op("v", lambda: g.vector.tensor_scalar(out, in0, s1, None, op0), r, w, ns)
        else: op("v", lambda: g.vector.tensor_scalar(out, in0, s1, s2, op0, op1), r, w, ns)

    def tt(out, in0, in1, how, r, w):
        op("v", lambda: g.vector.tensor_tensor(out, in0, in1, how), r, w, short(0))

    def act(out, in_, func, bias, scale, r, w, n, total=None):
        op("s", lambda: g.scalar.activation(out, in_, func, bias, scale, accum_out=total), r, w, (64 + n) * CYCLE)

    def fill(out, c, w, n=0):
        op("v", lambda: g.vector.memset(out, c), (), w, short(n))

    def count_up(out, pattern, base, w, n):
        op("g", lambda: g.iota(out, pattern, base, 0, allow_small_or_imprecise_dtypes=True), (), w, 130 + 2 * n * CYCLE)

    def turn(out, in_, r, w, n=0):
        op("v", lambda: g.vector.transpose(out, in_), r, w, short(n))

    def scan(out, d0, d1, init, op0, op1, r, w, n):
        op("v", lambda: g.vector.tensor_tensor_scan(out, d0, d1, init, op0, op1), r, w, short(n))

    def move(q, out, in_, r, w, ns):
        if q == "v": op("v", lambda: g.vector.tensor_copy(out, in_), r, w, ns)
        else: op("s", lambda: g.scalar.activation(out, in_, ACT.Copy), r, w, ns)

    def quant(name, c0, c1, in_, r, w):
        op("v", lambda: g.vector.quantize_mx(T[name + "q"][:, c0:c1], T[name + "p"][:, c0:c1], in_), r, w, 12 + 0.88 * (c1 - c0))

    def product(out, left, l0, right, c0, c1, r, w):
        op("t", lambda: g.tensor.matmul_mx(out, T[left + "q"][:, l0:l0 + 128], T[left + "p"][:, l0:l0 + 128],
                                           T[right + "q"][:, c0:c1], T[right + "p"][:, c0:c1], True, True), r, w, (c1 - c0 + 16) * CYCLE)

    def dma(q, out, in_, sem, r, w, ns, on=0):
        e = g.sync if q == "y" else g.scalar
        op(q, lambda: e.dma_start(out, in_), r, w, ns, sem, own=False, on=on)

    ps = [T["ps%d" % b] for b in range(8)]
    col = lambda i: T.cf[:, i:i + 1]
    num = lambda i: T.pi[:, i:i + 1]
    U1, SC, KB, XK, XF, XG, CP, SAME, Z1, Z2, Z3, MU, GA, BE = range(14)
    sends = rank < n_ranks - 1
    far = 100000

    dma("y", T.ub[:], T.u[:], "lu", [], ["ub"], 900, 6 * far)
    for h, (c0, c1) in enumerate(PIECES[0]):
        dma("y", T.xb[:, 4 * c0:4 * c1], T.x[:, 4 * c0:4 * c1], ("lx", "lx2")[h], [], ["xb%d" % h], 1400 + 350 * h, (5 - h) * far)
    dma("y", T.wq[:].bitcast(dt.uint8), T.wc[:], "lw", [], ["wq"], 2300, 3 * far)
    dma("y", T.wp[:], T.ws[:], "lp", [], ["wp"], 2400, 2 * far)
    dma("y", T.vb[:], T.v[:], "lv", [], ["vb"], 2700, far)

    op("g", lambda: g.iota(num(0), [[0, 1]], 0, 1), (), ["p"], 132)
    op("g", lambda: g.iota(num(7), [[0, 1]], 0, 16), (), ["p7"], 132)
    count_up(T.ui[:], [[32, 4], [-4, 2]], 4, ["ui"], 8)
    count_up(T.mv[:], [[0, 2], [-1, 32]], 0, ["mv"], 64)
    count_up(T.bt[:, 0:32], [[0, 32]], -1, ["bt"], 32)
    count_up(T.zi[:], [[8, 2]], 0, ["zi"], 2)
    for o in range(2):
        count_up(T.xe[:, X * o + M:X * o + X], [[0, K]], 0, ["xe2%d" % o], 32)
    count_up(T.tb[:], [[0, 64]], 0, ["tb"], 64)
    count_up(T.sel[:, 64 + 31::32], [[0, 33]], 0, ["sel0", "sel1"], 33)
    count_up(T.pw[:, C::W], [[0, 4]], 0, ["nil"], 4)
    count_up(T.ji[:], [[32, C // 32], [1, 16]], -C // 2, ["ji"], C // 2)
    count_up(T.z32[:], [[0, 32]], 0, ["z32"], 32)
    for t in range(R):
        count_up(T["inv%d" % t][:], [[0, L]], C // 2, ["inv%d" % t], L)
    if sends:
        count_up(T.et[:, 128:512], [[0, 384]], 0, ["et0"], 384)
    if rank > 0:
        count_up(T.one[:], [[0, 516]], 1, ["one"], 516)
        op("g", lambda: g.affine_select(T.one[:], T.one[:], [[-1, 516]], A.is_equal, 0.0, 3, 4), ["one"], ["one"], 170 + 1032 * CYCLE)

    ts(num(1), num(7), 16, None, A.bitwise_and, None, ["p7"], ["p1"])
    for i, s, m in ((2, 0, 15), (3, 0, 31), (4, 0, 1), (5, 4, 1), (6, 1, 7), (8, 2, 3)):
        if s: ts(num(i), num(0), s, m, A.logical_shift_right, A.bitwise_and, ["p"], ["p%d" % i])
        else: ts(num(i), num(0), m, None, A.bitwise_and, None, ["p"], ["p%d" % i])
    tt(col(U1), num(1), num(8), A.subtract, ["p1", "p8"], ["u1"])
    ts(T.ul[:], T.ui[:], col(U1), None, A.add, None, ["ui", "u1"], ["ul"])
    quant("t", 0, 128, T.ub[:], ["ub"], ["tq"])
    move("v", T.uq[:].bitcast(dt.uint32), T.tq[:].bitcast(dt.uint32).indirect(T.ul[:]), ["tq", "ul"], ["uq"], picked(128))
    move("s", T.up[:], T.tp[:].indirect(T.ul[:]), ["tq", "ul"], ["up"], picked(128))
    fill(T.on[:, K:X], 1.0, ["on"], M)
    fill(T.on[:, K - 1:K], UNIT, ["on1"])
    for o in range(2):
        act(T.zz[:, M * o:M * o + M], T.on[:, K:X], ACT.Copy, 0.0, -1.0, ["on"], ["zz%d" % o], M)
    act(T.dn[:], T.on[:, K:K + 256], ACT.Copy, 0.0, -1.0, ["on"], ["dn"], 256)
    for t in range(R):
        act(T["h%d" % t][:], T.on[:, K:K + L], ACT.Copy, 0.0, 0.5, ["on"], ["h%d" % t], L)
    for i, c in ((None, 2.0), (0, 0.0), (1, 1 / 16), (7, -0.5)):
        fill(T.hn[:] if i is None else T.hn[:, i::8], c, ["hn"])
    ts(col(XF), num(2), -1.0, None, A.mult, None, ["p2"], ["xf"])
    ts(col(XG), num(2), -1.0, -1.0, A.mult, A.add, ["p2"], ["xg"])
    ts(col(SC), num(3), 20.0, -1.0, A.is_lt, A.mult, ["p3"], ["sc"])
    ts(col(XK), num(3), 0.5, None, A.add, None, ["p3"], ["xk"])
    ts(col(KB), num(3), 2 * UNIT, -K * UNIT, A.mult, A.add, ["p3"], ["kb"])
    ts(col(CP), num(2), 15.0, 1 / LIFT, A.is_equal, A.max, ["p2"], ["cp"])
    ts(T.s16[:, 16:32], T.mv[:, 0:16], col(XF), None, A.not_equal, None, ["mv", "xf"], ["db"])
    ts(T.s16[:, 0:16], T.mv[:, 0:16], col(XG), LIFT, A.is_equal, A.mult, ["mv", "xg"], ["da"])
    ts(T.dl[:], T.mv[:, 0:26], 0.0, col(XF), A.mult, A.subtract, ["mv", "xf"], ["dl"])
    tt(T.s16[:, 32:48], T.s16[:, 0:16], T.s16[:, 16:32], A.max, ["da", "db"], ["dc"])
    move("s", T.dm[:], T.s16[:, 32:48].indirect(T.dl[:]), ["dc", "dl"], ["dm"], picked(L))
    for i, (c0, c1) in enumerate(((0, K), (L, L + 2 * K), (M + L, 2 * M))):
        ts(T.mt[:, c0:c1], T.mv[:, 0:c1 - c0], col(XK), None, A.add, None, ["mv", "xk"], ["mt%d" % i])
    for o in range(2):
        ts(T.xe[:, X * o + K:X * o + 2 * K], T.mt[:, 0:K], 0.5, 2 * UNIT, A.is_equal, A.mult, ["mt0"], ["xe0%d" % o])
    tt(col(SAME), num(4), num(5), A.is_equal, ["p4", "p5"], ["same"])
    ts(col(Z1), num(5), 528.0, 63.0, A.mult, A.add, ["p5"], ["z1"])
    ts(col(Z2), num(5), -16.0, 32.0, A.mult, A.add, ["p5"], ["z2"])
    ts(col(Z3), num(5), 512.0, 63.0, A.mult, A.add, ["p5"], ["z3"])
    ts(col(MU), col(SAME), 31.0, 1.0, A.mult, A.add, ["same"], ["mu"])
    ts(col(GA), col(Z1), col(SAME), col(Z2), A.mult, A.add, ["same", "z1", "z2"], ["ga"])
    ts(col(BE), num(6), col(MU), col(GA), A.mult, A.add, ["p6", "mu", "ga"], ["be"])
    ts(T.zl[:, 0:2], T.zi[:], col(MU), col(BE), A.mult, A.add, ["zi", "mu", "be"], ["zl"])
    ts(T.zl[:, 2:3], num(2), 32.0, col(Z3), A.mult, A.add, ["p2", "z3"], ["za"])
    ts(T.zl[:, 4:5], num(2), col(Z2), 1.0, A.add, A.add, ["p2", "z2"], ["zb"])
    ts(T.jv[:, 0:C // 2], T.ji[:], col(Z2), 32.0, A.subtract, A.add, ["ji", "z2"], ["ja"], short(C // 2))
    ts(T.jv[:, C // 2:C], T.ji[:], col(Z2), -16.0, A.add, A.add, ["ji", "z2"], ["jb"], short(C // 2))
    quant("v", 0, 128, T.vb[:], ["vb"], ["vq"])
    if rank > 0:
        fill(T.ct[:], 0.0, ["ct"], 512)
        for b in range(4):
            quant("i", 128 * b, 128 * b + 128, T.one[:, 3 - b:515 - b], ["one"], ["i%d" % b])
        quant("l", 96, 224, T.ct[:], ["ct"], ["lz"])
        if rank > 2:
            for s in range(2):
                fill(T.cm[:, K * s:K * s + K], 0.5 ** (2 - s), ["cm%d" % s])

    def state(t, h, tile, r):
        c0, c1 = PIECES[t][h]
        an, a = "a%d" % t, "a%d%d" % (t, h)
        quant(an, c0, c1, tile[:, 4 * c0:4 * c1], r, [a])
        if t < R:
            product(ps[h][:, 0:c1 - c0], "u", 0, an, c0, c1, ["uq", "up", a], ["ps%d" % h])
            act(T.b2[:, c0:c1], ps[h][:, 0:c1 - c0], ACT.Sign, -TINY, col(SC), ["sc"], ["ps%d" % h, "b2%d" % h], c1 - c0)
        else:
            product(ps[h][:, 0:c1 - c0], "v", 0, an, c0, c1, ["vq", a], ["ps%d" % h])
            dma("y", T.oc[:, 4 * c0:4 * c1], T[an + "q"][:, c0:c1].bitcast(dt.uint8), "oc", [a], [], 1000)
            if h:
                for k in range(4):
                    dma("ys"[k % 2], T.osc[4 * k:4 * k + 4, :], T[an + "p"][32 * k:32 * k + 4, :], ("oc", "oy")[k % 2], [an + "0", a], [], 800)
            move("sv"[h], T.yb[:, c0:c1], ps[h][:, 0:c1 - c0], [], ["ps%d" % h, "y%d" % h], (c1 - c0) * CYCLE)
            dma("s", T.y[:, c0:c1], T.yb[:, c0:c1], "oy", ["y%d" % h], [], 1000)

    calls = plan_calls(topo, cores, rank)
    sent = [0]

    def landing(t, d, s):
        return (96 - K * d if t == 0 else 224) + K * s

    def early(t, d, s):
        return t > 0 and s == 0 and d > 1

    def send(t):
        order = calls
        if t < R - 1:
            order = [[e for e in call if (e[0] == n_ranks - 1) == late] for late in (False, True) for call in calls]
        for call in [c for c in order if c]:
            for part in range(2):
                def issue(call=call, part=part):
                    tr = []
                    for d, es in call:
                        a = landing(t, d, rank)
                        rid, pid = topo.addr(cores[d])[0:2]
                        if part == 0:
                            src, dst = T["e%dq" % t][:, 0:K].bitcast(dt.uint8), T.lq[:, a:a + K].bitcast(dt.uint8)
                        else:
                            src, dst = T["e%dp" % t][:, 0:K], T.lp[:, a:a + K]
                        tr.append(RemoteDMATransfer(dst_ids=[DstId(rid=rid, pnc=pid)], dma_engine_mask=sum(1 << e for e in es),
                                                    remote_sem=T.sem["arr%d" % (t + early(t, d, rank))], src=src, dst=dst))
                        sent[0] += len(es)
                    g.remote_dma_fused(tr, local_sem=T.sem.sent)
                op("g", issue, ["e%d" % t], ["calls"], 200, on=(R - t) * 20000 * (rank == 0))

    def arriving(t, soon):
        return 2 * sum(len(es) for s in range(rank) for call in plan_calls(topo, cores, s) for d, es in call
                       if d == rank and early(t, d, s) == soon)

    slots, ends = T.pl[:, 0:2], T.pl[:, 26:28]
    plane = lambda buf, b: buf[:, L * b:L * b + L]

    def one_round(t):
        an, a = "a%d" % t, ["a%d0" % t, "a%d1" % t]
        half, hk, inv, ik = T["h%d" % t], "h%d" % t, T["inv%d" % t], "inv%d" % t
        for b in range(4):
            product(ps[4 + b][:, 0:C], "w", 128 * b, an, 0, C, ["wq", "wp"] + a, ["ps%d" % (4 + b)])
            act(T.pw[:, W * b:W * b + C], ps[4 + b][:, 0:C], ACT.Copy, 0.0, 0.03125, [], ["ps%d" % (4 + b), "pw%d" % b], C)
        for h, (c0, c1) in enumerate(PIECES[t]):
            n = c1 - c0
            turn(T.bt[:, K + c0:K + c1], T.b2[:, c0:c1], ["b2%d" % h], ["bt%d" % h], n)
            for o in range(2):
                z, oh = M * o + c0 + K * h, "%d%d" % (o, h)
                scan(T.zz[:, z + 4:z + 4 + n:4], T.hn[:, 0:n // 4], T.bt[:, K - 8 + c0 + o:K - 8 + c1:4], 0.0, A.mult, A.add,
                     ["hn", "zz%d" % o, "bt", "bt0", "bt%d" % h], ["zz" + oh], 0)
                scan(T.mt[:, M * o + K + c0:M * o + K + c1], T.dn[:, 0:n], T.zz[:, z + K:z + K + n], 0.0, A.add, A.max,
                     ["dn", "zz%d" % o, "zz" + oh], ["mt" + oh], n)
                mk = T.mk[:, C * o + c0:C * o + c1]
                turn(mk, T.mt[:, M * o + K + c0:M * o + K + c1], ["mt" + oh], ["mk" + oh], n)
                ts(T.xe[:, X * o + 2 * K + c0:X * o + 2 * K + c1], mk, 0.5, 2 * UNIT, A.is_equal, A.mult, ["mk" + oh], ["xe1" + oh], short(n))
                act(T.sg[:, C * o + c0:C * o + c1], mk, ACT.Sign, 0.0, -1.0, ["mk" + oh], ["sg" + oh, "acc" + oh], n + 24,
                    T.acc[:, 2 * o + h:2 * o + h + 1])
        for o in range(2):
            ts(T.xe[:, X * o + K - 1:X * o + K], T.acc[:, 2 * o:2 * o + 1], UNIT, col(KB), A.mult, A.add, ["kb", "acc%d0" % o], ["xl%d" % o])
            scan(T.cu[:, X * o + K - 1:X * o + X], T.on[:, K - 1:X], T.xe[:, X * o + K - 1:X * o + X], T.acc[:, 2 * o + 1:2 * o + 2], A.mult, A.add,
                 ["on", "on1", "xl%d" % o, "xe0%d" % o, "xe1%d0" % o, "xe1%d1" % o, "xe2%d" % o, "acc%d1" % o], ["cu%d" % o], M)
            turn(T.st[:, M * o:M * o + M], T.cu[:, X * o + K:X * o + X], ["cu%d" % o], ["st%d" % o], M)
            scan(T.sel[:, 64 + 512 * o:64 + 512 * o + M], T.mt[:, M * o:M * o + M], T.st[:, M * o:M * o + M], 0.0, A.max, A.min,
                 ["mt0", "mt1", "mt2", "mt%d0" % o, "mt%d1" % o, "st%d" % o], ["sel%d" % o], M)
        turn(T.tb[:, 16:48], T.sel[:, 64 + 31:64 + 1024:32], ["sel0", "sel1"], ["tb"])
        turn(T.sel[:, 0:64], T.tb[:], ["tb"], ["sel2"])

        def places(out, c0, c1, lst, r, w, n):
            ts(out, T.sel[:, c0:c1].indirect(lst), 0.5 / UNIT, L / 2 - 1.0, A.mult, A.add, r, w, picked(n))

        places(T.pa[:, 0:16], 64, 1120, T.zl[:, 2:3], ["za", "sel0", "sel1"], ["pa"], 16)
        places(T.pa[:, 16:32], 0, 64, T.zl[:, 4:5], ["zb", "sel2"], ["pb"], 16)
        places(T.pl[:], 0, 1120, T.zl[:, 0:2], ["zl", "sel0", "sel1", "sel2"], ["pl"], 32)
        for i, r in enumerate("ab"):
            move("v", inv[:].indirect(T.pa[:, 16 * i:16 * i + 12]), T.jv[:, 192 * i:192 * i + 192], ["p" + r, "j" + r], [ik], spread(192))
        move("v", half[:].indirect(slots), T.z32[:], ["pl", "z32"], [hk], spread(K))
        scan(T.dg[:], T.dm[:], inv[:], 0.0, A.mult, A.add, ["dm", ik], ["dg"], L)
        ts(T.il[:], T.dg[:, 15::16], col(CP), C / 2, A.mult, A.add, ["dg", "cp"], ["il"])

        made = {b: [] for b in range(4)}
        for b, q, c0, c1 in SORT:
            made[b].append("pz%d_%d" % (b, len(made[b])))
            move(q, T.pz[:, L * b + 16 * c0:L * b + 16 * c1], T.pw[:, W * b:W * b + W].indirect(T.il[:, c0:c1]),
                 ["il", "nil", "pw%d" % b], [made[b][-1]], picked(16 * (c1 - c0)))

        def run(b):
            scan(plane(T.hs, b), half[:], plane(T.pz, b), 0.0, A.mult, A.max, [hk] + made[b], ["hs%d" % b], L)

        if sends:
            for b in (2, 0, 1, 3):
                run(b)
                move("sssv"[b], T.et[:, b:128:4], plane(T.hs, b).indirect(ends), ["pl", "hs%d" % b], ["et1%d" % b], picked(K))
            quant("e%d" % t, 0, 128, T.et[:], ["et0"] + ["et1%d" % b for b in range(4)], ["e%d" % t])
            send(t)

        if rank > 0:
            def unpack(b, v0, r):
                product(ps[b][:, 0:128], "i", 128 * b, "l", v0, v0 + 128, ["i%d" % b, "lz"] + r, ["ps%d" % b])

            soon = early(t, rank, 0)
            if soon:
                op(None, None, a, ["soon"], 3000, "arr%d" % (t + 1), arriving(t, True), False)
                for b in range(4):
                    unpack(b, landing(t, rank, 0) - 96, ["soon"])
                    act(T.d2[:, K * b:K * b + K], ps[b][:, 96:128], ACT.Copy, 0.0, 0.5 ** (rank - 1), [], ["ps%d" % b, "d2%d" % b], K)
            op(None, None, ["e%d" % t] if sends else [made[b][-1] for b in range(4)], ["land%d" % t], 2000 if sends else 3500,
               "arr%d" % t, arriving(t, False), False)
            v0 = 96 - K * rank if t == 0 else 96 + K * rank
            end = lambda b, s, n=1: ps[b][:, landing(t, rank, s) - v0:landing(t, rank, s) - v0 + K * n]
            for b in range(4):
                unpack(b, v0, ["land%d" % t, "soon"])
                out, pb, d0, d1, d2 = T.ct[:, b:128:4], "ps%d" % b, T.dd[:, 64 * b:64 * b + K], T.dd[:, 64 * b + K:64 * b + 64], T.d2[:, K * b:K * b + K]
                if rank == 1:
                    move("v", out, end(b, 0), ["ct"], [pb, "ct%d" % b], short(0))
                elif rank == 2 and soon:
                    tt(out, d2, end(b, 1), A.max, ["ct", "d2%d" % b], [pb, "ct%d" % b])
                elif rank == 2:
                    ts(d0, end(b, 0), 0.5, None, A.mult, None, [], [pb, "dd%d" % b])
                    tt(out, d0, end(b, 1), A.max, ["ct", "dd%d" % b], [pb, "ct%d" % b])
                elif soon:
                    ts(d0, end(b, 1), 0.5, None, A.mult, None, [], [pb, "dd%d" % b])
                    tt(d1, d2, end(b, 2), A.max, ["d2%d" % b], [pb, "de%d" % b])
                    tt(out, d0, d1, A.max, ["ct", "dd%d" % b, "de%d" % b], ["ct%d" % b])
                else:
                    tt(T.dd[:, 64 * b:64 * b + 64], end(b, 0, 2), T.cm[:], A.mult, ["cm0", "cm1"], [pb, "dd%d" % b, "de%d" % b])
                    tt(d2, d0, end(b, 2), A.max, ["dd%d" % b], [pb, "d2%d" % b])
                    tt(out, d1, d2, A.max, ["ct", "de%d" % b, "d2%d" % b], ["ct%d" % b])
            quant("c", 0, 128, T.ct[:], ["ct"] + ["ct%d" % b for b in range(4)], ["cq"])
            for b in range(4):
                product(ps[4 + b][:, 0:128], "i", 128 * b, "c", 0, 128, ["i%d" % b, "cq"], ["ps%d" % (4 + b)])
                move("s", T.cc[:, K * b:K * b + K], ps[4 + b][:, 0:K], [], ["ps%d" % (4 + b), "cc%d" % b], 96 * CYCLE)
                move("v", plane(T.pz, b).indirect(slots), T.cc[:, K * b:K * b + K], ["pl", "cc%d" % b], made[b], spread(K))
                run(b)
        for h, (c0, c1) in enumerate(PIECES[t + 1]):
            for b in range(4):
                move(UNSORT[t][h][b], T.ht[:, 4 * c0 + b:4 * c1:4], plane(T.hs, b).indirect(T.pl[:, 2 + c0 // 16:2 + c1 // 16]),
                     ["pl", "hs%d" % b], ["ht%d%d" % (b, h)], picked(c1 - c0))
            state(t + 1, h, T.ht, ["ht%d%d" % (b, h) for b in range(4)])

    for h in range(2):
        state(0, h, T.xb, ["xb%d" % h])
    for t in range(R):
        one_round(t)

    count = emit(g, T, ops)
    g.sync.wait_ge(T.sem.oc, count["oc"])
    g.scalar.wait_ge(T.sem.oy, count["oy"])
    if sent[0]:
        g.wait_ge(T.sem.sent, sent[0])
